import numpy as np
import ml_dtypes


def mxq(x, axis, fmt="e4m3"):
    dtype, down = {"e4m3": (ml_dtypes.float8_e4m3fn, 7), "e5m2": (ml_dtypes.float8_e5m2, 14)}[fmt]
    v = np.moveaxis(np.asarray(x, np.float32).astype(ml_dtypes.bfloat16).astype(np.float64), axis, -1)
    blocks = v.reshape(v.shape[:-1] + (-1, 32))
    amax = np.abs(blocks).max(-1, keepdims=True)
    byte = np.maximum(np.where(amax > 0, np.frexp(amax)[1] - 1 + 127, 0) - down, 1)
    scale = np.exp2(byte - 127.0)
    codes = (blocks / scale).astype(np.float32).astype(dtype).astype(np.float64)
    return np.moveaxis((codes * scale).reshape(v.shape), -1, axis)


WIDE = False


def mx_kscale(k):
    if not WIDE:
        return np.ones(k)
    levels = np.array([10, -10, 5, -5, 0])
    if k % 512:
        return np.exp2(np.random.permutation(np.resize(levels, k // 32))).repeat(32)
    a = np.empty((k // 512, 16))
    for p in range(k // 512):
        a[p, :8] = np.random.permutation(np.resize(levels, 8))
        for g in range(8):
            far = levels[np.abs(levels - a[p, g]) >= 10]
            a[p, g + 8] = far[np.random.randint(len(far))]
    return np.exp2(a.ravel()).repeat(32)


def f64(x):
    return np.asarray(x).astype(np.float64)


def striped(idx):
    return np.tile(idx.reshape(-1, 16).T, (8, 1)).astype(np.uint16)


def unstriped(offs):
    return offs[:16].T.reshape(-1).astype(np.int64)


K, T, S, N, U = 512, 1024, 512, 256, 1024


def setup_inputs():
    n = np.random.standard_normal
    s = mx_kscale(K)[:, None]
    return {
        "xT": (n((K, T)) * s).astype(np.float32),
        "mem": n((N, U)).astype(np.float32),
        "w1": (n((K, N)) / np.sqrt(K) / s).astype(np.float32),
        "offs": striped(np.random.permutation(T)[:S]),
        "slot": striped(np.random.permutation(U)[:S]),
    }


def reference(xT, mem, w1, offs, slot):
    xq = mxq(f64(xT)[:, unstriped(offs)], 0, "e4m3")
    y = mxq(f64(w1), 0, "e4m3").T @ xq
    out = f64(mem).copy()
    out[:, unstriped(slot)] = np.maximum(f64(mem)[:, unstriped(slot)], y)
    return out

@@ -1,0 +1,100 @@
+from contextlib import ExitStack
+
+import concourse.mybir as mybir
+
+K, T, S, N, U = 512, 1024, 512, 256, 1024
+FLOPS = 2 * K * S * N
+
+F32 = mybir.dt.float32
+BF16 = mybir.dt.bfloat16
+U32 = mybir.dt.uint32
+U16 = mybir.dt.uint16
+U8 = mybir.dt.uint8
+FP8X4 = mybir.dt.float8_e4m3fn_x4
+
+P = 128
+PACK = 4
+BLOCKS = N // P
+HALVES = 2
+HALF = S // HALVES
+LIST_COLS = S // 16
+HALF_COLS = HALF // 16
+
+
+def tile_picked_idxput_max_e_kernel(tc, xT, mem, w1, offs, slot, out):
+    nc = tc.nc
+    with ExitStack() as ctx:
+        lists = ctx.enter_context(tc.tile_pool(name="lists", bufs=1))
+        keep = ctx.enter_context(tc.tile_pool(name="keep", bufs=1))
+        psum = ctx.enter_context(tc.psum_pool(name="psum", bufs=1))
+
+        offs_sb = lists.tile([P, LIST_COLS], U16, name="offs_sb")
+        slot_sb = lists.tile([P, LIST_COLS], U16, name="slot_sb")
+        x_rows = xT.rearrange("(p t) c -> p t c", t=PACK)
+        x_plane = [keep.tile([P, T], F32, name=f"x_plane{t}") for t in range(PACK)]
+        store = [keep.tile([P, U], F32, name=f"store{b}") for b in range(BLOCKS)]
+        w_raw = keep.tile([P, PACK, N], F32, name="w_raw")
+
+        nc.sync.dma_start(x_plane[0][:], x_rows[:, 0, :])
+        nc.sync.dma_start(offs_sb[:], offs)
+        for t in range(1, PACK):
+            nc.sync.dma_start(x_plane[t][:], x_rows[:, t, :])
+        nc.sync.dma_start(slot_sb[:], slot)
+        for b in range(BLOCKS):
+            nc.sync.dma_start(store[b][:], mem[b * P : (b + 1) * P, :])
+        nc.sync.dma_start(w_raw[:], w1.rearrange("(p t) n -> p t n", t=PACK))
+
+        picked = [keep.tile([P, PACK, HALF], BF16, name=f"picked{h}") for h in range(HALVES)]
+        for t in range(PACK):
+            for h in range(HALVES):
+                nc.vector.tensor_copy(
+                    picked[h][:, t, :],
+                    x_plane[t][:].indirect(offs_sb[:, h * HALF_COLS : (h + 1) * HALF_COLS]),
+                )
+        x_grouped = [keep.tile([P, HALF, PACK], BF16, name=f"x_grouped{h}", align_bytes=64) for h in range(HALVES)]
+        for h in range(HALVES):
+            nc.scalar.copy(x_grouped[h][:], picked[h][:].rearrange("p t j -> p j t"))
+
+        old = [keep.tile([P, S], F32, name=f"old{b}") for b in range(BLOCKS)]
+        for b in range(BLOCKS):
+            nc.vector.tensor_copy(old[b][:], store[b][:].indirect(slot_sb[:]))
+
+        x_codes = [keep.tile([P, HALF], U32, name=f"x_codes{h}", align_bytes=64) for h in range(HALVES)]
+        x_scales = [keep.tile([P, HALF], U8, name=f"x_scales{h}", align_bytes=64) for h in range(HALVES)]
+        for h in range(HALVES):
+            nc.vector.quantize_mx(
+                out=x_codes[h][:].bitcast(FP8X4),
+                scales=x_scales[h][:],
+                in_=x_grouped[h][:].rearrange("p j t -> p (j t)"),
+            )
+
+        y = []
+        for b in range(BLOCKS):
+            w_grouped = keep.tile([P, P, PACK], BF16, name=f"w_grouped{b}", align_bytes=64)
+            nc.scalar.copy(w_grouped[:], w_raw[:, :, b * P : (b + 1) * P].rearrange("p t n -> p n t"))
+            w_codes = keep.tile([P, P], U32, name=f"w_codes{b}", align_bytes=64)
+            w_scales = keep.tile([P, P], U8, name=f"w_scales{b}", align_bytes=64)
+            nc.vector.quantize_mx(
+                out=w_codes[:].bitcast(FP8X4),
+                scales=w_scales[:],
+                in_=w_grouped[:].rearrange("p n t -> p (n t)"),
+            )
+            bank = psum.tile([P, S], F32, name=f"y{b}")
+            for h in range(HALVES):
+                nc.tensor.matmul_mx(
+                    out=bank[:, h * HALF : (h + 1) * HALF],
+                    lhsT=w_codes[:].bitcast(FP8X4),
+                    lhsT_scale=w_scales[:],
+                    rhs=x_codes[h][:].bitcast(FP8X4),
+                    rhs_scale=x_scales[h][:],
+                    start=True,
+                    stop=True,
+                )
+            y.append(bank)
+
+        new = [keep.tile([P, S], F32, name=f"new{b}") for b in range(BLOCKS)]
+        for b in range(BLOCKS):
+            nc.vector.tensor_tensor(new[b][:], y[b][:], old[b][:], mybir.AluOpType.max)
+        for b in range(BLOCKS):
+            nc.vector.tensor_copy(store[b][:].indirect(slot_sb[:]), new[b][:])
+            nc.sync.dma_start(out[b * P : (b + 1) * P, :], store[b][:])

@@ -37,62 +37,71 @@ def tile_picked_idxput_max_e_kernel(tc, xT, mem, w1, offs, slot, out):
 
         nc.sync.dma_start(x_plane[0][:], x_rows[:, 0, :])
         nc.sync.dma_start(offs_sb[:], offs)
+        nc.sync.dma_start(slot_sb[:], slot)
         for t in range(1, PACK):
             nc.sync.dma_start(x_plane[t][:], x_rows[:, t, :])
-        nc.sync.dma_start(slot_sb[:], slot)
-        for b in range(BLOCKS):
-            nc.sync.dma_start(store[b][:], mem[b * P : (b + 1) * P, :])
+        nc.sync.dma_start(store[0][:], mem[0:P, :])
         nc.sync.dma_start(w_raw[:], w1.rearrange("(p t) n -> p t n", t=PACK))
+        nc.sync.dma_start(store[1][:], mem[P : 2 * P, :])
 
-        picked = [keep.tile([P, PACK, HALF], BF16, name=f"picked{h}") for h in range(HALVES)]
-        for t in range(PACK):
-            for h in range(HALVES):
-                nc.vector.tensor_copy(
-                    picked[h][:, t, :],
-                    x_plane[t][:].indirect(offs_sb[:, h * HALF_COLS : (h + 1) * HALF_COLS]),
-                )
-        x_grouped = [keep.tile([P, HALF, PACK], BF16, name=f"x_grouped{h}", align_bytes=64) for h in range(HALVES)]
+        picked = keep.tile([P, PACK, S], BF16, name="picked")
+        x_grouped = keep.tile([P, S, PACK], BF16, name="x_grouped", align_bytes=64)
+        x_codes = keep.tile([P, S], U32, name="x_codes", align_bytes=64)
+        x_scales = keep.tile([P, S], U8, name="x_scales", align_bytes=64)
+        old = [keep.tile([P, S], F32, name="old0")]
+        new = [keep.tile([P, S], F32, name=f"new{b}") for b in range(BLOCKS)]
+        halves = [slice(h * HALF, (h + 1) * HALF) for h in range(HALVES)]
+
+        for t in range(PACK - 1):
+            nc.vector.tensor_copy(picked[:, t, :], x_plane[t][:].indirect(offs_sb[:]))
         for h in range(HALVES):
-            nc.scalar.copy(x_grouped[h][:], picked[h][:].rearrange("p t j -> p j t"))
-
-        old = [keep.tile([P, S], F32, name=f"old{b}") for b in range(BLOCKS)]
-        for b in range(BLOCKS):
-            nc.vector.tensor_copy(old[b][:], store[b][:].indirect(slot_sb[:]))
-
-        x_codes = [keep.tile([P, HALF], U32, name=f"x_codes{h}", align_bytes=64) for h in range(HALVES)]
-        x_scales = [keep.tile([P, HALF], U8, name=f"x_scales{h}", align_bytes=64) for h in range(HALVES)]
-        for h in range(HALVES):
-            nc.vector.quantize_mx(
-                out=x_codes[h][:].bitcast(FP8X4),
-                scales=x_scales[h][:],
-                in_=x_grouped[h][:].rearrange("p j t -> p (j t)"),
+            nc.vector.tensor_copy(
+                picked[:, PACK - 1, halves[h]],
+                x_plane[PACK - 1][:].indirect(offs_sb[:, h * HALF_COLS : (h + 1) * HALF_COLS]),
             )
+        nc.scalar.copy(x_grouped[:, :, 0:2], picked[:, 0:2, :].rearrange("p t j -> p j t"))
+        for cols in halves:
+            nc.scalar.copy(x_grouped[:, cols, 2:4], picked[:, 2:4, cols].rearrange("p t j -> p j t"))
 
-        y = []
-        for b in range(BLOCKS):
-            w_grouped = keep.tile([P, P, PACK], BF16, name=f"w_grouped{b}", align_bytes=64)
-            nc.scalar.copy(w_grouped[:], w_raw[:, :, b * P : (b + 1) * P].rearrange("p t n -> p n t"))
+        nc.vector.tensor_copy(old[0][:], store[0][:].indirect(slot_sb[:]))
+        nc.vector.quantize_mx(
+            out=x_codes[:].bitcast(FP8X4),
+            scales=x_scales[:],
+            in_=x_grouped[:].rearrange("p j t -> p (j t)"),
+        )
+
+        w_grouped = [
+            keep.tile([P, P, PACK], BF16, name=f"w_grouped{b}", tag=f"w_grouped{b}", align_bytes=64)
+            for b in range(BLOCKS)
+        ]
+        for b in reversed(range(BLOCKS)):
+            nc.scalar.copy(
+                w_grouped[b][:].rearrange("p (c i) t -> p c t i", i=2),
+                w_raw[:, :, b * P : (b + 1) * P].rearrange("p t (c i) -> p c t i", i=2),
+            )
+        y = {}
+        for b in reversed(range(BLOCKS)):
             w_codes = keep.tile([P, P], U32, name=f"w_codes{b}", align_bytes=64)
             w_scales = keep.tile([P, P], U8, name=f"w_scales{b}", align_bytes=64)
             nc.vector.quantize_mx(
                 out=w_codes[:].bitcast(FP8X4),
                 scales=w_scales[:],
-                in_=w_grouped[:].rearrange("p n t -> p (n t)"),
+                in_=w_grouped[b][:].rearrange("p n t -> p (n t)"),
             )
             bank = psum.tile([P, S], F32, name=f"y{b}")
-            for h in range(HALVES):
-                nc.tensor.matmul_mx(
-                    out=bank[:, h * HALF : (h + 1) * HALF],
-                    lhsT=w_codes[:].bitcast(FP8X4),
-                    lhsT_scale=w_scales[:],
-                    rhs=x_codes[h][:].bitcast(FP8X4),
-                    rhs_scale=x_scales[h][:],
-                    start=True,
-                    stop=True,
-                )
-            y.append(bank)
+            nc.tensor.matmul_mx(
+                out=bank[:],
+                lhsT=w_codes[:].bitcast(FP8X4),
+                lhsT_scale=w_scales[:],
+                rhs=x_codes[:].bitcast(FP8X4),
+                rhs_scale=x_scales[:],
+                start=True,
+                stop=True,
+            )
+            y[b] = bank
 
-        new = [keep.tile([P, S], F32, name=f"new{b}") for b in range(BLOCKS)]
+        old.append(keep.tile([P, S], F32, name="old1", tag="w_grouped0", align_bytes=64))
+        nc.vector.tensor_copy(old[1][:], store[1][:].indirect(slot_sb[:]))
         for b in range(BLOCKS):
             nc.vector.tensor_tensor(new[b][:], y[b][:], old[b][:], mybir.AluOpType.max)
         for b in range(BLOCKS):

@@ -19,6 +19,7 @@ HALVES = 2
 HALF = S // HALVES
 LIST_COLS = S // 16
 HALF_COLS = HALF // 16
+W_SPLIT = 48
 
 
 def tile_picked_idxput_max_e_kernel(tc, xT, mem, w1, offs, slot, out):
@@ -64,20 +65,25 @@ def tile_picked_idxput_max_e_kernel(tc, xT, mem, w1, offs, slot, out):
             nc.scalar.copy(x_grouped[:, cols, 2:4], picked[:, 2:4, cols].rearrange("p t j -> p j t"))
 
         nc.vector.tensor_copy(old[0][:], store[0][:].indirect(slot_sb[:]))
-        nc.vector.quantize_mx(
-            out=x_codes[:].bitcast(FP8X4),
-            scales=x_scales[:],
-            in_=x_grouped[:].rearrange("p j t -> p (j t)"),
-        )
+        for cols in halves:
+            nc.vector.quantize_mx(
+                out=x_codes[:, cols].bitcast(FP8X4),
+                scales=x_scales[:, cols],
+                in_=x_grouped[:, cols, :].rearrange("p j t -> p (j t)"),
+            )
 
         w_grouped = [
             keep.tile([P, P, PACK], BF16, name=f"w_grouped{b}", tag=f"w_grouped{b}", align_bytes=64)
             for b in range(BLOCKS)
         ]
-        for b in reversed(range(BLOCKS)):
-            nc.scalar.copy(
-                w_grouped[b][:].rearrange("p (c i) t -> p c t i", i=2),
-                w_raw[:, :, b * P : (b + 1) * P].rearrange("p t (c i) -> p c t i", i=2),
+        for copy, b, first, last in (
+            (nc.scalar.copy, 1, 0, P),
+            (nc.scalar.copy, 0, 0, W_SPLIT),
+            (nc.vector.tensor_copy, 0, W_SPLIT, P),
+        ):
+            copy(
+                w_grouped[b][:, first:last, :].rearrange("p (c i) t -> p c t i", i=2),
+                w_raw[:, :, b * P + first : b * P + last].rearrange("p t (c i) -> p c t i", i=2),
             )
         y = {}
         for b in reversed(range(BLOCKS)):
@@ -100,7 +106,7 @@ def tile_picked_idxput_max_e_kernel(tc, xT, mem, w1, offs, slot, out):
             )
             y[b] = bank
 
-        old.append(keep.tile([P, S], F32, name="old1", tag="w_grouped0", align_bytes=64))
+        old.append(keep.tile([P, S], F32, name="old1", tag="w_grouped1", align_bytes=64))
         nc.vector.tensor_copy(old[1][:], store[1][:].indirect(slot_sb[:]))
         for b in range(BLOCKS):
             nc.vector.tensor_tensor(new[b][:], y[b][:], old[b][:], mybir.AluOpType.max)

@@ -19,7 +19,6 @@ HALVES = 2
 HALF = S // HALVES
 LIST_COLS = S // 16
 HALF_COLS = HALF // 16
-W_SPLIT = 48
 
 
 def tile_picked_idxput_max_e_kernel(tc, xT, mem, w1, offs, slot, out):
@@ -50,7 +49,6 @@ def tile_picked_idxput_max_e_kernel(tc, xT, mem, w1, offs, slot, out):
         x_codes = keep.tile([P, S], U32, name="x_codes", align_bytes=64)
         x_scales = keep.tile([P, S], U8, name="x_scales", align_bytes=64)
         old = [keep.tile([P, S], F32, name="old0")]
-        new = [keep.tile([P, S], F32, name=f"new{b}") for b in range(BLOCKS)]
         halves = [slice(h * HALF, (h + 1) * HALF) for h in range(HALVES)]
 
         for t in range(PACK - 1):
@@ -76,14 +74,10 @@ def tile_picked_idxput_max_e_kernel(tc, xT, mem, w1, offs, slot, out):
             keep.tile([P, P, PACK], BF16, name=f"w_grouped{b}", tag=f"w_grouped{b}", align_bytes=64)
             for b in range(BLOCKS)
         ]
-        for copy, b, first, last in (
-            (nc.scalar.copy, 1, 0, P),
-            (nc.scalar.copy, 0, 0, W_SPLIT),
-            (nc.vector.tensor_copy, 0, W_SPLIT, P),
-        ):
-            copy(
-                w_grouped[b][:, first:last, :].rearrange("p (c i) t -> p c t i", i=2),
-                w_raw[:, :, b * P + first : b * P + last].rearrange("p t (c i) -> p c t i", i=2),
+        for b in reversed(range(BLOCKS)):
+            nc.scalar.copy(
+                w_grouped[b][:].rearrange("p (c i) t -> p c t i", i=2),
+                w_raw[:, :, b * P : (b + 1) * P].rearrange("p t (c i) -> p c t i", i=2),
             )
         y = {}
         for b in reversed(range(BLOCKS)):
@@ -106,10 +100,17 @@ def tile_picked_idxput_max_e_kernel(tc, xT, mem, w1, offs, slot, out):
             )
             y[b] = bank
 
-        old.append(keep.tile([P, S], F32, name="old1", tag="w_grouped1", align_bytes=64))
-        nc.vector.tensor_copy(old[1][:], store[1][:].indirect(slot_sb[:]))
-        for b in range(BLOCKS):
-            nc.vector.tensor_tensor(new[b][:], y[b][:], old[b][:], mybir.AluOpType.max)
-        for b in range(BLOCKS):
-            nc.vector.tensor_copy(store[b][:].indirect(slot_sb[:]), new[b][:])
-            nc.sync.dma_start(out[b * P : (b + 1) * P, :], store[b][:])
+        old.append(keep.tile([P, S], F32, name="old1"))
+        for h in range(HALVES):
+            nc.vector.tensor_copy(
+                old[1][:, halves[h]], store[1][:].indirect(slot_sb[:, h * HALF_COLS : (h + 1) * HALF_COLS])
+            )
+        new = [keep.tile([P, S], F32, name=f"new{b}") for b in range(BLOCKS)]
+        for cols in halves:
+            nc.vector.tensor_tensor(new[1][:, cols], y[1][:, cols], old[1][:, cols], mybir.AluOpType.max)
+        nc.vector.tensor_copy(store[1][:].indirect(slot_sb[:, 0:HALF_COLS]), new[1][:, halves[0]])
+        nc.vector.tensor_tensor(new[0][:], y[0][:], old[0][:], mybir.AluOpType.max)
+        nc.vector.tensor_copy(store[1][:].indirect(slot_sb[:, HALF_COLS:LIST_COLS]), new[1][:, halves[1]])
+        nc.sync.dma_start(out[P : 2 * P, :], store[1][:])
+        nc.vector.tensor_copy(store[0][:].indirect(slot_sb[:]), new[0][:])
+        nc.sync.dma_start(out[0:P, :], store[0][:])

@@ -19,6 +19,7 @@ HALVES = 2
 HALF = S // HALVES
 LIST_COLS = S // 16
 HALF_COLS = HALF // 16
+LAST_PLANE_PARTS = ((0, 128), (128, 320), (320, 512))
 
 
 def tile_picked_idxput_max_e_kernel(tc, xT, mem, w1, offs, slot, out):
@@ -51,19 +52,24 @@ def tile_picked_idxput_max_e_kernel(tc, xT, mem, w1, offs, slot, out):
         old = [keep.tile([P, S], F32, name="old0")]
         halves = [slice(h * HALF, (h + 1) * HALF) for h in range(HALVES)]
 
-        for t in range(PACK - 1):
-            nc.vector.tensor_copy(picked[:, t, :], x_plane[t][:].indirect(offs_sb[:]))
+        nc.vector.tensor_copy(picked[:, 0, :], x_plane[0][:].indirect(offs_sb[:]))
         for h in range(HALVES):
             nc.vector.tensor_copy(
-                picked[:, PACK - 1, halves[h]],
-                x_plane[PACK - 1][:].indirect(offs_sb[:, h * HALF_COLS : (h + 1) * HALF_COLS]),
+                picked[:, 1, halves[h]], x_plane[1][:].indirect(offs_sb[:, h * HALF_COLS : (h + 1) * HALF_COLS])
             )
-        nc.scalar.copy(x_grouped[:, :, 0:2], picked[:, 0:2, :].rearrange("p t j -> p j t"))
+        nc.vector.tensor_copy(picked[:, 2, :], x_plane[2][:].indirect(offs_sb[:]))
+        for first, last in LAST_PLANE_PARTS:
+            nc.vector.tensor_copy(
+                picked[:, PACK - 1, first:last],
+                x_plane[PACK - 1][:].indirect(offs_sb[:, first // 16 : last // 16]),
+            )
         for cols in halves:
-            nc.scalar.copy(x_grouped[:, cols, 2:4], picked[:, 2:4, cols].rearrange("p t j -> p j t"))
+            nc.scalar.copy(x_grouped[:, cols, 0:2], picked[:, 0:2, cols].rearrange("p t j -> p j t"))
+        for first, last in LAST_PLANE_PARTS:
+            nc.scalar.copy(x_grouped[:, first:last, 2:4], picked[:, 2:4, first:last].rearrange("p t j -> p j t"))
 
         nc.vector.tensor_copy(old[0][:], store[0][:].indirect(slot_sb[:]))
-        for cols in halves:
+        for cols in [slice(0, S)]:
             nc.vector.quantize_mx(
                 out=x_codes[:, cols].bitcast(FP8X4),
                 scales=x_scales[:, cols],

@@ -19,7 +19,8 @@ HALVES = 2
 HALF = S // HALVES
 LIST_COLS = S // 16
 HALF_COLS = HALF // 16
-LAST_PLANE_PARTS = ((0, 128), (128, 320), (320, 512))
+LAST_PLANE_PARTS = ((0, 128), (128, 256), (256, 384))
+SHARE = 128
 
 
 def tile_picked_idxput_max_e_kernel(tc, xT, mem, w1, offs, slot, out):
@@ -52,21 +53,45 @@ def tile_picked_idxput_max_e_kernel(tc, xT, mem, w1, offs, slot, out):
         old = [keep.tile([P, S], F32, name="old0")]
         halves = [slice(h * HALF, (h + 1) * HALF) for h in range(HALVES)]
 
-        nc.vector.tensor_copy(picked[:, 0, :], x_plane[0][:].indirect(offs_sb[:]))
-        for h in range(HALVES):
+        def gather(t, first, last):
             nc.vector.tensor_copy(
-                picked[:, 1, halves[h]], x_plane[1][:].indirect(offs_sb[:, h * HALF_COLS : (h + 1) * HALF_COLS])
+                picked[:, t, first:last], x_plane[t][:].indirect(offs_sb[:, first // 16 : last // 16])
             )
-        nc.vector.tensor_copy(picked[:, 2, :], x_plane[2][:].indirect(offs_sb[:]))
-        for first, last in LAST_PLANE_PARTS:
-            nc.vector.tensor_copy(
-                picked[:, PACK - 1, first:last],
-                x_plane[PACK - 1][:].indirect(offs_sb[:, first // 16 : last // 16]),
-            )
-        for cols in halves:
-            nc.scalar.copy(x_grouped[:, cols, 0:2], picked[:, 0:2, cols].rearrange("p t j -> p j t"))
-        for first, last in LAST_PLANE_PARTS:
-            nc.scalar.copy(x_grouped[:, first:last, 2:4], picked[:, 2:4, first:last].rearrange("p t j -> p j t"))
+
+        def place(planes, first, last):
+            nc.scalar.copy(x_grouped[:, first:last, planes], picked[:, planes, first:last].rearrange("p t j -> p j t"))
+
+        own = S - SHARE
+        last_rounded = keep.tile([P, T], BF16, name="last_rounded")
+        gather(0, 0, S)
+        gather(1, 0, HALF)
+        place(slice(0, 2), 0, HALF)
+        gather(1, HALF, S)
+        place(slice(0, 2), HALF, own)
+        gather(2, own, S)
+        place(slice(0, 3), own, S)
+        gather(2, 0, own)
+        nc.gpsimd.tensor_scalar(
+            last_rounded[:], x_plane[3][:], 1.0, 0.0, op0=mybir.AluOpType.mult, op1=mybir.AluOpType.add
+        )
+        for first, last in LAST_PLANE_PARTS[:-1]:
+            gather(3, first, last)
+            place(slice(2, 4), first, last)
+        first, last = LAST_PLANE_PARTS[-1]
+        gather(3, first, last)
+        nc.gpsimd.tensor_scalar(
+            x_grouped[:, first:last, 2:4],
+            picked[:, 2:4, first:last].rearrange("p t j -> p j t"),
+            1.0,
+            0.0,
+            op0=mybir.AluOpType.mult,
+            op1=mybir.AluOpType.add,
+        )
+        nc.scalar.activation(
+            x_grouped[:, own:S, 3],
+            last_rounded[:].indirect(offs_sb[:, own // 16 : LIST_COLS]),
+            mybir.ActivationFunctionType.Copy,
+        )
 
         nc.vector.tensor_copy(old[0][:], store[0][:].indirect(slot_sb[:]))
         for cols in [slice(0, S)]:

@@ -19,8 +19,8 @@ HALVES = 2
 HALF = S // HALVES
 LIST_COLS = S // 16
 HALF_COLS = HALF // 16
-LAST_PLANE_PARTS = ((0, 128), (128, 256), (256, 384))
-SHARE = 128
+LAST_PLANE_PARTS = ((0, 128), (128, 320))
+SHARE = 192
 
 
 def tile_picked_idxput_max_e_kernel(tc, xT, mem, w1, offs, slot, out):

@@ -21,6 +21,7 @@ LIST_COLS = S // 16
 HALF_COLS = HALF // 16
 LAST_PLANE_PARTS = ((0, 128), (128, 320))
 SHARE = 192
+W_SPLIT = 80
 
 
 def tile_picked_idxput_max_e_kernel(tc, xT, mem, w1, offs, slot, out):
@@ -35,16 +36,18 @@ def tile_picked_idxput_max_e_kernel(tc, xT, mem, w1, offs, slot, out):
         x_rows = xT.rearrange("(p t) c -> p t c", t=PACK)
         x_plane = [keep.tile([P, T], F32, name=f"x_plane{t}") for t in range(PACK)]
         store = [keep.tile([P, U], F32, name=f"store{b}") for b in range(BLOCKS)]
-        w_raw = keep.tile([P, PACK, N], F32, name="w_raw")
+        w_raw = [keep.tile([P, PACK, P], F32, name=f"w_raw{b}") for b in range(BLOCKS)]
 
+        w_rows = w1.rearrange("(p t) n -> p t n", t=PACK)
         nc.sync.dma_start(x_plane[0][:], x_rows[:, 0, :])
         nc.sync.dma_start(offs_sb[:], offs)
         nc.sync.dma_start(slot_sb[:], slot)
         for t in range(1, PACK):
             nc.sync.dma_start(x_plane[t][:], x_rows[:, t, :])
         nc.sync.dma_start(store[0][:], mem[0:P, :])
-        nc.sync.dma_start(w_raw[:], w1.rearrange("(p t) n -> p t n", t=PACK))
+        nc.sync.dma_start(w_raw[1][:], w_rows[:, :, P : 2 * P])
         nc.sync.dma_start(store[1][:], mem[P : 2 * P, :])
+        nc.sync.dma_start(w_raw[0][:], w_rows[:, :, 0:P])
 
         picked = keep.tile([P, PACK, S], BF16, name="picked")
         x_grouped = keep.tile([P, S, PACK], BF16, name="x_grouped", align_bytes=64)
@@ -72,8 +75,9 @@ def tile_picked_idxput_max_e_kernel(tc, xT, mem, w1, offs, slot, out):
         place(slice(0, 3), own, S)
         gather(2, 0, own)
         nc.gpsimd.tensor_scalar(
-            last_rounded[:], x_plane[3][:], 1.0, 0.0, op0=mybir.AluOpType.mult, op1=mybir.AluOpType.add
+            last_rounded[:, 0:704], x_plane[3][:, 0:704], 1.0, 0.0, op0=mybir.AluOpType.mult, op1=mybir.AluOpType.add
         )
+        nc.scalar.copy(last_rounded[:, 704:T], x_plane[3][:, 704:T])
         for first, last in LAST_PLANE_PARTS[:-1]:
             gather(3, first, last)
             place(slice(2, 4), first, last)
@@ -105,11 +109,19 @@ def tile_picked_idxput_max_e_kernel(tc, xT, mem, w1, offs, slot, out):
             keep.tile([P, P, PACK], BF16, name=f"w_grouped{b}", tag=f"w_grouped{b}", align_bytes=64)
             for b in range(BLOCKS)
         ]
-        for b in reversed(range(BLOCKS)):
+        for b, last in ((1, P), (0, W_SPLIT)):
             nc.scalar.copy(
-                w_grouped[b][:].rearrange("p (c i) t -> p c t i", i=2),
-                w_raw[:, :, b * P : (b + 1) * P].rearrange("p t (c i) -> p c t i", i=2),
+                w_grouped[b][:, 0:last, :].rearrange("p (c i) t -> p c t i", i=2),
+                w_raw[b][:, :, 0:last].rearrange("p t (c i) -> p c t i", i=2),
             )
+        nc.gpsimd.tensor_scalar(
+            w_grouped[0][:, W_SPLIT:P, :].rearrange("p (c i) t -> p c t i", i=2),
+            w_raw[0][:, :, W_SPLIT:P].rearrange("p t (c i) -> p c t i", i=2),
+            1.0,
+            0.0,
+            op0=mybir.AluOpType.mult,
+            op1=mybir.AluOpType.add,
+        )
         y = {}
         for b in reversed(range(BLOCKS)):
             w_codes = keep.tile([P, P], U32, name=f"w_codes{b}", align_bytes=64)
@@ -136,7 +148,7 @@ def tile_picked_idxput_max_e_kernel(tc, xT, mem, w1, offs, slot, out):
             nc.vector.tensor_copy(
                 old[1][:, halves[h]], store[1][:].indirect(slot_sb[:, h * HALF_COLS : (h + 1) * HALF_COLS])
             )
-        new = [keep.tile([P, S], F32, name=f"new{b}") for b in range(BLOCKS)]
+        new = [keep.tile([P, S], F32, name="new0"), keep.tile([P, S], F32, name="new1", tag="w_raw0")]
         for cols in halves:
             nc.vector.tensor_tensor(new[1][:, cols], y[1][:, cols], old[1][:, cols], mybir.AluOpType.max)
         nc.vector.tensor_copy(store[1][:].indirect(slot_sb[:, 0:HALF_COLS]), new[1][:, halves[0]])

@@ -22,6 +22,7 @@ HALF_COLS = HALF // 16
 LAST_PLANE_PARTS = ((0, 128), (128, 320))
 SHARE = 192
 W_SPLIT = 80
+LOWEST = -3.4028234663852886e38
 
 
 def tile_picked_idxput_max_e_kernel(tc, xT, mem, w1, offs, slot, out):
@@ -131,29 +132,59 @@ def tile_picked_idxput_max_e_kernel(tc, xT, mem, w1, offs, slot, out):
                 scales=w_scales[:],
                 in_=w_grouped[b][:].rearrange("p n t -> p (n t)"),
             )
-            bank = psum.tile([P, S], F32, name=f"y{b}")
-            nc.tensor.matmul_mx(
-                out=bank[:],
-                lhsT=w_codes[:].bitcast(FP8X4),
-                lhsT_scale=w_scales[:],
-                rhs=x_codes[:].bitcast(FP8X4),
-                rhs_scale=x_scales[:],
-                start=True,
-                stop=True,
-            )
-            y[b] = bank
+            for cols in halves if b == 0 else [slice(0, S)]:
+                bank = psum.tile([P, cols.stop - cols.start], F32, name=f"y{b}_{cols.start}")
+                nc.tensor.matmul_mx(
+                    out=bank[:],
+                    lhsT=w_codes[:].bitcast(FP8X4),
+                    lhsT_scale=w_scales[:],
+                    rhs=x_codes[:, cols].bitcast(FP8X4),
+                    rhs_scale=x_scales[:, cols],
+                    start=True,
+                    stop=True,
+                )
+                y[b, cols.start] = bank
 
         old.append(keep.tile([P, S], F32, name="old1"))
         for h in range(HALVES):
             nc.vector.tensor_copy(
                 old[1][:, halves[h]], store[1][:].indirect(slot_sb[:, h * HALF_COLS : (h + 1) * HALF_COLS])
             )
-        new = [keep.tile([P, S], F32, name="new0"), keep.tile([P, S], F32, name="new1", tag="w_raw0")]
+        direct = S - 256
+        new = [keep.tile([P, direct], F32, name="new0"), keep.tile([P, S], F32, name="new1", tag="w_raw0")]
         for cols in halves:
-            nc.vector.tensor_tensor(new[1][:, cols], y[1][:, cols], old[1][:, cols], mybir.AluOpType.max)
-        nc.vector.tensor_copy(store[1][:].indirect(slot_sb[:, 0:HALF_COLS]), new[1][:, halves[0]])
-        nc.vector.tensor_tensor(new[0][:], y[0][:], old[0][:], mybir.AluOpType.max)
-        nc.vector.tensor_copy(store[1][:].indirect(slot_sb[:, HALF_COLS:LIST_COLS]), new[1][:, halves[1]])
+            nc.vector.tensor_tensor(new[1][:, cols], y[1, 0][:, cols], old[1][:, cols], mybir.AluOpType.max)
+
+        rest = S - direct
+        kept = keep.tile([P, rest], F32, name="kept", tag="w_grouped0", align_bytes=64)
+        nc.gpsimd.tensor_scalar(
+            kept[:], old[0][:, direct:S], float("inf"), LOWEST, op0=mybir.AluOpType.min, op1=mybir.AluOpType.max
+        )
+        update = keep.tile([P, rest], F32, name="update")
+        nc.scalar.copy(update[:], y[0, HALF][:])
+        gap = keep.tile([P, rest], F32, name="gap")
+        nc.gpsimd.tensor_tensor(gap[:], kept[:], update[:], mybir.AluOpType.subtract)
+        side = keep.tile([P, rest], F32, name="side")
+        nc.scalar.activation(side[:], gap[:], mybir.ActivationFunctionType.Sign)
+        kept_share = keep.tile([P, rest], F32, name="kept_share")
+        update_share = keep.tile([P, rest], F32, name="update_share")
+        nc.scalar.activation(kept_share[:], side[:], mybir.ActivationFunctionType.Copy, bias=0.5, scale=0.5)
+        nc.scalar.activation(update_share[:], side[:], mybir.ActivationFunctionType.Copy, bias=0.5, scale=-0.5)
+        kept_part = keep.tile([P, rest], F32, name="kept_part")
+        update_part = keep.tile([P, rest], F32, name="update_part")
+        nc.gpsimd.tensor_tensor(kept_part[:], kept[:], kept_share[:], mybir.AluOpType.mult)
+        nc.gpsimd.tensor_tensor(update_part[:], update[:], update_share[:], mybir.AluOpType.mult)
+
+        def put(b, first, last):
+            nc.vector.tensor_copy(store[b][:].indirect(slot_sb[:, first // 16 : last // 16]), new[b][:, first:last])
+
+        put(1, 0, 192)
+        nc.vector.tensor_tensor(new[0][:], y[0, 0][:], old[0][:, 0:direct], mybir.AluOpType.max)
+        put(1, 192, 352)
+        put(0, 0, direct)
+        put(1, 352, S)
         nc.sync.dma_start(out[P : 2 * P, :], store[1][:])
-        nc.vector.tensor_copy(store[0][:].indirect(slot_sb[:]), new[0][:])
+        nc.vector.tensor_tensor(
+            store[0][:].indirect(slot_sb[:, direct // 16 : LIST_COLS]), kept_part[:], update_part[:], mybir.AluOpType.add
+        )
         nc.sync.dma_start(out[0:P, :], store[0][:])

@@ -21,7 +21,7 @@ LIST_COLS = S // 16
 HALF_COLS = HALF // 16
 LAST_PLANE_PARTS = ((0, 128), (128, 320))
 SHARE = 192
-W_SPLIT = 80
+W_SPLIT = 96
 LOWEST = -3.4028234663852886e38
 
 
@@ -76,9 +76,9 @@ def tile_picked_idxput_max_e_kernel(tc, xT, mem, w1, offs, slot, out):
         place(slice(0, 3), own, S)
         gather(2, 0, own)
         nc.gpsimd.tensor_scalar(
-            last_rounded[:, 0:704], x_plane[3][:, 0:704], 1.0, 0.0, op0=mybir.AluOpType.mult, op1=mybir.AluOpType.add
+            last_rounded[:, 0:544], x_plane[3][:, 0:544], 1.0, 0.0, op0=mybir.AluOpType.mult, op1=mybir.AluOpType.add
         )
-        nc.scalar.copy(last_rounded[:, 704:T], x_plane[3][:, 704:T])
+        nc.scalar.copy(last_rounded[:, 544:T], x_plane[3][:, 544:T])
         for first, last in LAST_PLANE_PARTS[:-1]:
             gather(3, first, last)
             place(slice(2, 4), first, last)
@@ -132,7 +132,7 @@ def tile_picked_idxput_max_e_kernel(tc, xT, mem, w1, offs, slot, out):
                 scales=w_scales[:],
                 in_=w_grouped[b][:].rearrange("p n t -> p (n t)"),
             )
-            for cols in halves if b == 0 else [slice(0, S)]:
+            for cols in halves[::-1] if b == 0 else [slice(0, S)]:
                 bank = psum.tile([P, cols.stop - cols.start], F32, name=f"y{b}_{cols.start}")
                 nc.tensor.matmul_mx(
                     out=bank[:],

@@ -40,15 +40,15 @@ def tile_picked_idxput_max_e_kernel(tc, xT, mem, w1, offs, slot, out):
         w_raw = [keep.tile([P, PACK, P], F32, name=f"w_raw{b}") for b in range(BLOCKS)]
 
         w_rows = w1.rearrange("(p t) n -> p t n", t=PACK)
-        nc.sync.dma_start(x_plane[0][:], x_rows[:, 0, :])
+        nc.scalar.dma_start(x_plane[0][:], x_rows[:, 0, :])
         nc.sync.dma_start(offs_sb[:], offs)
         nc.sync.dma_start(slot_sb[:], slot)
         for t in range(1, PACK):
-            nc.sync.dma_start(x_plane[t][:], x_rows[:, t, :])
-        nc.sync.dma_start(store[0][:], mem[0:P, :])
-        nc.sync.dma_start(w_raw[1][:], w_rows[:, :, P : 2 * P])
-        nc.sync.dma_start(store[1][:], mem[P : 2 * P, :])
-        nc.sync.dma_start(w_raw[0][:], w_rows[:, :, 0:P])
+            nc.scalar.dma_start(x_plane[t][:], x_rows[:, t, :])
+        nc.scalar.dma_start(store[0][:], mem[0:P, :])
+        nc.scalar.dma_start(w_raw[1][:], w_rows[:, :, P : 2 * P])
+        nc.scalar.dma_start(store[1][:], mem[P : 2 * P, :])
+        nc.scalar.dma_start(w_raw[0][:], w_rows[:, :, 0:P])
 
         picked = keep.tile([P, PACK, S], BF16, name="picked")
         x_grouped = keep.tile([P, S, PACK], BF16, name="x_grouped", align_bytes=64)
@@ -145,7 +145,7 @@ def tile_picked_idxput_max_e_kernel(tc, xT, mem, w1, offs, slot, out):
                 )
                 y[b, cols.start] = bank
 
-        old.append(keep.tile([P, S], F32, name="old1"))
+        old.append(keep.tile([P, S], F32, name="old1", tag="w_raw1"))
         for h in range(HALVES):
             nc.vector.tensor_copy(
                 old[1][:, halves[h]], store[1][:].indirect(slot_sb[:, h * HALF_COLS : (h + 1) * HALF_COLS])

@@ -11,18 +11,13 @@ U32 = mybir.dt.uint32
 U16 = mybir.dt.uint16
 U8 = mybir.dt.uint8
 FP8X4 = mybir.dt.float8_e4m3fn_x4
+COPY = mybir.ActivationFunctionType.Copy
+MAX = mybir.AluOpType.max
 
 P = 128
 PACK = 4
-BLOCKS = N // P
-HALVES = 2
-HALF = S // HALVES
-LIST_COLS = S // 16
-HALF_COLS = HALF // 16
-LAST_PLANE_PARTS = ((0, 128), (128, 320))
-SHARE = 192
-W_SPLIT = 96
-LOWEST = -3.4028234663852886e38
+HALF = S // 2
+PIECE = 128
 
 
 def tile_picked_idxput_max_e_kernel(tc, xT, mem, w1, offs, slot, out):
@@ -32,159 +27,135 @@ def tile_picked_idxput_max_e_kernel(tc, xT, mem, w1, offs, slot, out):
         keep = ctx.enter_context(tc.tile_pool(name="keep", bufs=1))
         psum = ctx.enter_context(tc.psum_pool(name="psum", bufs=1))
 
-        offs_sb = lists.tile([P, LIST_COLS], U16, name="offs_sb")
-        slot_sb = lists.tile([P, LIST_COLS], U16, name="slot_sb")
+        offs_sb = lists.tile([P, S // 16], U16, name="offs_sb")
+        slot_sb = lists.tile([P, S // 16], U16, name="slot_sb")
+        x_plane = [keep.tile([P, T], F32, name=f"x_plane{t}", tag=f"x_plane{t}", align_bytes=64) for t in range(PACK)]
+        store = [keep.tile([P, U], F32, name=f"store{b}") for b in range(2)]
+        work = keep.tile([P, 1152], F32, name="work")
+        old_first = work[:, 128:640]
+        old_vector = work[:, 640:896]
+        old_scalar = work[:, 0:256]
+        new = keep.tile([P, 2 * S], F32, name="new")
+        w_raw0 = keep.tile([P, PACK, P], F32, name="w_raw0")
+        w_raw = [w_raw0[:], work[:, 640:1152].rearrange("p (t n) -> p t n", t=PACK)]
+
         x_rows = xT.rearrange("(p t) c -> p t c", t=PACK)
-        x_plane = [keep.tile([P, T], F32, name=f"x_plane{t}") for t in range(PACK)]
-        store = [keep.tile([P, U], F32, name=f"store{b}") for b in range(BLOCKS)]
-        w_raw = [keep.tile([P, PACK, P], F32, name=f"w_raw{b}") for b in range(BLOCKS)]
-
         w_rows = w1.rearrange("(p t) n -> p t n", t=PACK)
-        nc.scalar.dma_start(x_plane[0][:], x_rows[:, 0, :])
         nc.sync.dma_start(offs_sb[:], offs)
+        for t in range(PACK):
+            nc.sync.dma_start(x_plane[t][:], x_rows[:, t, :])
         nc.sync.dma_start(slot_sb[:], slot)
-        for t in range(1, PACK):
-            nc.scalar.dma_start(x_plane[t][:], x_rows[:, t, :])
-        nc.scalar.dma_start(store[0][:], mem[0:P, :])
-        nc.scalar.dma_start(w_raw[1][:], w_rows[:, :, P : 2 * P])
-        nc.scalar.dma_start(store[1][:], mem[P : 2 * P, :])
-        nc.scalar.dma_start(w_raw[0][:], w_rows[:, :, 0:P])
+        for b in range(2):
+            nc.sync.dma_start(w_raw[b], w_rows[:, :, b * P : (b + 1) * P])
+            nc.sync.dma_start(store[b][:], mem[b * P : (b + 1) * P, :])
 
-        picked = keep.tile([P, PACK, S], BF16, name="picked")
-        x_grouped = keep.tile([P, S, PACK], BF16, name="x_grouped", align_bytes=64)
-        x_codes = keep.tile([P, S], U32, name="x_codes", align_bytes=64)
-        x_scales = keep.tile([P, S], U8, name="x_scales", align_bytes=64)
-        old = [keep.tile([P, S], F32, name="old0")]
-        halves = [slice(h * HALF, (h + 1) * HALF) for h in range(HALVES)]
+        warm = keep.tile([P, 2], F32, name="warm")
+        nc.gpsimd.memset(warm[:, 0:1], 0.0)
+        nc.scalar.activation(warm[:, 1:2], warm[:, 0:1], COPY)
 
-        def gather(t, first, last):
-            nc.vector.tensor_copy(
-                picked[:, t, first:last], x_plane[t][:].indirect(offs_sb[:, first // 16 : last // 16])
-            )
+        def entries(list_sb, first, last):
+            return list_sb[:, first // 16 : last // 16]
 
-        def place(planes, first, last):
-            nc.scalar.copy(x_grouped[:, first:last, planes], picked[:, planes, first:last].rearrange("p t j -> p j t"))
-
-        own = S - SHARE
-        last_rounded = keep.tile([P, T], BF16, name="last_rounded")
-        gather(0, 0, S)
-        gather(1, 0, HALF)
-        place(slice(0, 2), 0, HALF)
-        gather(1, HALF, S)
-        place(slice(0, 2), HALF, own)
-        gather(2, own, S)
-        place(slice(0, 3), own, S)
-        gather(2, 0, own)
+        x_grouped = [
+            keep.tile([P, HALF, PACK], BF16, name=f"x_grouped{h}", tag=f"x_grouped{h}", align_bytes=64) for h in range(2)
+        ]
+        picked_early = keep.tile([P, 2 * HALF], BF16, name="picked_early")
+        picked = [picked_early[:], work[:, 192:448].bitcast(BF16)]
+        for t in range(PACK):
+            pair, plane = divmod(t, 2)
+            parts = ((0, PIECE), (PIECE, HALF)) if t == PACK - 1 else ((0, HALF),)
+            for first, last in parts:
+                nc.vector.tensor_copy(x_grouped[0][:, first:last, t], x_plane[t][:].indirect(entries(offs_sb, first, last)))
+            for first, last in parts:
+                nc.scalar.activation(
+                    picked[pair][:, plane * HALF + first : plane * HALF + last],
+                    x_plane[t][:].indirect(entries(offs_sb, HALF + first, HALF + last)),
+                    COPY,
+                )
+            if t == 1:
+                nc.gpsimd.tensor_scalar(
+                    x_grouped[1][:, :, 0:2],
+                    picked[0].rearrange("p (t j) -> p j t", t=2),
+                    1.0,
+                    0.0,
+                    op0=mybir.AluOpType.mult,
+                    op1=mybir.AluOpType.add,
+                )
+        late = picked[1].rearrange("p (t j) -> p j t", t=2)
         nc.gpsimd.tensor_scalar(
-            last_rounded[:, 0:544], x_plane[3][:, 0:544], 1.0, 0.0, op0=mybir.AluOpType.mult, op1=mybir.AluOpType.add
+            x_grouped[1][:, 0:PIECE, 2:4], late[:, 0:PIECE, :], 1.0, 0.0, op0=mybir.AluOpType.mult, op1=mybir.AluOpType.add
         )
-        nc.scalar.copy(last_rounded[:, 544:T], x_plane[3][:, 544:T])
-        for first, last in LAST_PLANE_PARTS[:-1]:
-            gather(3, first, last)
-            place(slice(2, 4), first, last)
-        first, last = LAST_PLANE_PARTS[-1]
-        gather(3, first, last)
-        nc.gpsimd.tensor_scalar(
-            x_grouped[:, first:last, 2:4],
-            picked[:, 2:4, first:last].rearrange("p t j -> p j t"),
-            1.0,
-            0.0,
-            op0=mybir.AluOpType.mult,
-            op1=mybir.AluOpType.add,
-        )
-        nc.scalar.activation(
-            x_grouped[:, own:S, 3],
-            last_rounded[:].indirect(offs_sb[:, own // 16 : LIST_COLS]),
-            mybir.ActivationFunctionType.Copy,
-        )
-
-        nc.vector.tensor_copy(old[0][:], store[0][:].indirect(slot_sb[:]))
-        for cols in [slice(0, S)]:
-            nc.vector.quantize_mx(
-                out=x_codes[:, cols].bitcast(FP8X4),
-                scales=x_scales[:, cols],
-                in_=x_grouped[:, cols, :].rearrange("p j t -> p (j t)"),
-            )
+        nc.scalar.copy(x_grouped[1][:, PIECE:HALF, 2:4], late[:, PIECE:HALF, :])
 
         w_grouped = [
-            keep.tile([P, P, PACK], BF16, name=f"w_grouped{b}", tag=f"w_grouped{b}", align_bytes=64)
-            for b in range(BLOCKS)
+            keep.tile([P, P, PACK], BF16, name=f"w_grouped{b}", tag=tag, align_bytes=64)
+            for b, tag in enumerate(("x_plane3", "x_grouped1"))
         ]
-        for b, last in ((1, P), (0, W_SPLIT)):
-            nc.scalar.copy(
-                w_grouped[b][:, 0:last, :].rearrange("p (c i) t -> p c t i", i=2),
-                w_raw[b][:, :, 0:last].rearrange("p t (c i) -> p c t i", i=2),
+        w_codes = [keep.tile([P, P], U32, name=f"w_codes{b}", align_bytes=64) for b in range(2)]
+        w_scales = [keep.tile([P, P], U8, name=f"w_scales{b}", align_bytes=64) for b in range(2)]
+        x_codes = [keep.tile([P, HALF], U32, name=f"x_codes{h}", align_bytes=64) for h in range(2)]
+        x_scales = [keep.tile([P, HALF], U8, name=f"x_scales{h}", align_bytes=64) for h in range(2)]
+
+        def quantize(codes, scales, grouped):
+            nc.vector.quantize_mx(out=codes.bitcast(FP8X4), scales=scales, in_=grouped.rearrange("p j t -> p (j t)"))
+
+        def product(bank, column, b, first, last):
+            h, start = divmod(first, HALF)
+            cols = slice(start, start + last - first)
+            nc.tensor.matmul_mx(
+                out=bank[:, column : column + last - first],
+                lhsT=w_codes[b][:].bitcast(FP8X4),
+                lhsT_scale=w_scales[b][:],
+                rhs=x_codes[h][:, cols].bitcast(FP8X4),
+                rhs_scale=x_scales[h][:, cols],
+                start=True,
+                stop=True,
             )
+
+        def larger(bank, first, old):
+            nc.vector.tensor_tensor(new[:, first : first + old.shape[1]], bank, old, MAX)
+
+        banks = [psum.tile([P, width], F32, name=f"y{i}") for i, width in enumerate((128, 256, 256, 384))]
+
+        nc.vector.tensor_copy(
+            w_grouped[0][:].rearrange("p (c i) t -> p c t i", i=4), w_raw[0].rearrange("p t (c i) -> p c t i", i=4)
+        )
+        quantize(x_codes[0][:], x_scales[0][:], x_grouped[0][:])
+        quantize(w_codes[0][:], w_scales[0][:], w_grouped[0][:])
+        quantize(x_codes[1][:], x_scales[1][:], x_grouped[1][:])
+        product(banks[0], 0, 0, 0, 128)
+        product(banks[1], 0, 0, 128, 256)
+        product(banks[1], 128, 0, 256, 384)
+        product(banks[2], 0, 0, 384, 512)
+
+        nc.vector.tensor_copy(old_first[:, 0:128], store[0][:].indirect(entries(slot_sb, 0, 128)))
+        nc.vector.tensor_copy(old_first[:, 128:256], store[0][:].indirect(entries(slot_sb, 128, 256)))
+        nc.scalar.activation(old_first[:, 256:S], store[0][:].indirect(entries(slot_sb, 256, S)), COPY)
+        larger(banks[0][:], 0, old_first[:, 0:128])
+        nc.scalar.activation(store[0][:].indirect(entries(slot_sb, 0, 128)), new[:, 0:128], COPY)
+        larger(banks[1][:], 128, old_first[:, 128:384])
+
         nc.gpsimd.tensor_scalar(
-            w_grouped[0][:, W_SPLIT:P, :].rearrange("p (c i) t -> p c t i", i=2),
-            w_raw[0][:, :, W_SPLIT:P].rearrange("p t (c i) -> p c t i", i=2),
+            w_grouped[1][:],
+            w_raw[1].rearrange("p t n -> p n t"),
             1.0,
             0.0,
             op0=mybir.AluOpType.mult,
             op1=mybir.AluOpType.add,
         )
-        y = {}
-        for b in reversed(range(BLOCKS)):
-            w_codes = keep.tile([P, P], U32, name=f"w_codes{b}", align_bytes=64)
-            w_scales = keep.tile([P, P], U8, name=f"w_scales{b}", align_bytes=64)
-            nc.vector.quantize_mx(
-                out=w_codes[:].bitcast(FP8X4),
-                scales=w_scales[:],
-                in_=w_grouped[b][:].rearrange("p n t -> p (n t)"),
-            )
-            for cols in halves[::-1] if b == 0 else [slice(0, S)]:
-                bank = psum.tile([P, cols.stop - cols.start], F32, name=f"y{b}_{cols.start}")
-                nc.tensor.matmul_mx(
-                    out=bank[:],
-                    lhsT=w_codes[:].bitcast(FP8X4),
-                    lhsT_scale=w_scales[:],
-                    rhs=x_codes[:, cols].bitcast(FP8X4),
-                    rhs_scale=x_scales[:, cols],
-                    start=True,
-                    stop=True,
-                )
-                y[b, cols.start] = bank
+        quantize(w_codes[1][:], w_scales[1][:], w_grouped[1][:])
+        product(banks[2], 128, 1, 0, 128)
+        product(banks[3], 0, 1, 128, 256)
+        product(banks[3], 128, 1, 256, 512)
 
-        old.append(keep.tile([P, S], F32, name="old1", tag="w_raw1"))
-        for h in range(HALVES):
-            nc.vector.tensor_copy(
-                old[1][:, halves[h]], store[1][:].indirect(slot_sb[:, h * HALF_COLS : (h + 1) * HALF_COLS])
-            )
-        direct = S - 256
-        new = [keep.tile([P, direct], F32, name="new0"), keep.tile([P, S], F32, name="new1", tag="w_raw0")]
-        for cols in halves:
-            nc.vector.tensor_tensor(new[1][:, cols], y[1, 0][:, cols], old[1][:, cols], mybir.AluOpType.max)
-
-        rest = S - direct
-        kept = keep.tile([P, rest], F32, name="kept", tag="w_grouped0", align_bytes=64)
-        nc.gpsimd.tensor_scalar(
-            kept[:], old[0][:, direct:S], float("inf"), LOWEST, op0=mybir.AluOpType.min, op1=mybir.AluOpType.max
-        )
-        update = keep.tile([P, rest], F32, name="update")
-        nc.scalar.copy(update[:], y[0, HALF][:])
-        gap = keep.tile([P, rest], F32, name="gap")
-        nc.gpsimd.tensor_tensor(gap[:], kept[:], update[:], mybir.AluOpType.subtract)
-        side = keep.tile([P, rest], F32, name="side")
-        nc.scalar.activation(side[:], gap[:], mybir.ActivationFunctionType.Sign)
-        kept_share = keep.tile([P, rest], F32, name="kept_share")
-        update_share = keep.tile([P, rest], F32, name="update_share")
-        nc.scalar.activation(kept_share[:], side[:], mybir.ActivationFunctionType.Copy, bias=0.5, scale=0.5)
-        nc.scalar.activation(update_share[:], side[:], mybir.ActivationFunctionType.Copy, bias=0.5, scale=-0.5)
-        kept_part = keep.tile([P, rest], F32, name="kept_part")
-        update_part = keep.tile([P, rest], F32, name="update_part")
-        nc.gpsimd.tensor_tensor(kept_part[:], kept[:], kept_share[:], mybir.AluOpType.mult)
-        nc.gpsimd.tensor_tensor(update_part[:], update[:], update_share[:], mybir.AluOpType.mult)
-
-        def put(b, first, last):
-            nc.vector.tensor_copy(store[b][:].indirect(slot_sb[:, first // 16 : last // 16]), new[b][:, first:last])
-
-        put(1, 0, 192)
-        nc.vector.tensor_tensor(new[0][:], y[0, 0][:], old[0][:, 0:direct], mybir.AluOpType.max)
-        put(1, 192, 352)
-        put(0, 0, direct)
-        put(1, 352, S)
-        nc.sync.dma_start(out[P : 2 * P, :], store[1][:])
-        nc.vector.tensor_tensor(
-            store[0][:].indirect(slot_sb[:, direct // 16 : LIST_COLS]), kept_part[:], update_part[:], mybir.AluOpType.add
-        )
+        nc.vector.tensor_copy(old_vector[:, 0:128], store[1][:].indirect(entries(slot_sb, 0, 128)))
+        nc.vector.tensor_copy(old_vector[:, 128:256], store[1][:].indirect(entries(slot_sb, 128, 256)))
+        nc.scalar.activation(old_scalar, store[1][:].indirect(entries(slot_sb, 256, S)), COPY)
+        larger(banks[2][:], 384, work[:, 512:768])
+        nc.scalar.activation(store[0][:].indirect(entries(slot_sb, 128, S)), new[:, 128:S], COPY)
         nc.sync.dma_start(out[0:P, :], store[0][:])
+        larger(banks[3][:, 0:128], S + 128, old_vector[:, 128:256])
+        larger(banks[3][:, 128:384], S + 256, old_scalar)
+        nc.vector.tensor_copy(store[1][:].indirect(entries(slot_sb, 0, 128)), new[:, S : S + 128])
+        nc.vector.tensor_copy(store[1][:].indirect(entries(slot_sb, 128, S)), new[:, S + 128 : 2 * S])
+        nc.sync.dma_start(out[P : 2 * P, :], store[1][:])

@@ -16,8 +16,10 @@ MAX = mybir.AluOpType.max
 
 P = 128
 PACK = 4
-HALF = S // 2
 PIECE = 128
+DIRECT = 288
+STAGED = S - DIRECT
+VECTOR_SECOND = 256
 
 
 def tile_picked_idxput_max_e_kernel(tc, xT, mem, w1, offs, slot, out):
@@ -29,133 +31,120 @@ def tile_picked_idxput_max_e_kernel(tc, xT, mem, w1, offs, slot, out):
 
         offs_sb = lists.tile([P, S // 16], U16, name="offs_sb")
         slot_sb = lists.tile([P, S // 16], U16, name="slot_sb")
-        x_plane = [keep.tile([P, T], F32, name=f"x_plane{t}", tag=f"x_plane{t}", align_bytes=64) for t in range(PACK)]
+        x_plane = [keep.tile([P, T], F32, name=f"x_plane{t}") for t in range(PACK)]
         store = [keep.tile([P, U], F32, name=f"store{b}") for b in range(2)]
-        work = keep.tile([P, 1152], F32, name="work")
-        old_first = work[:, 128:640]
-        old_vector = work[:, 640:896]
-        old_scalar = work[:, 0:256]
+        old = keep.tile([P, 2 * S], F32, name="old")
         new = keep.tile([P, 2 * S], F32, name="new")
-        w_raw0 = keep.tile([P, PACK, P], F32, name="w_raw0")
-        w_raw = [w_raw0[:], work[:, 640:1152].rearrange("p (t n) -> p t n", t=PACK)]
+        w_raw_first = keep.tile([P, PACK, P], F32, name="w_raw_first")
+        w_raw = [w_raw_first[:], new[:, PIECE : PIECE + S].rearrange("p (t n) -> p t n", t=PACK)]
 
         x_rows = xT.rearrange("(p t) c -> p t c", t=PACK)
         w_rows = w1.rearrange("(p t) n -> p t n", t=PACK)
         nc.sync.dma_start(offs_sb[:], offs)
+        nc.sync.dma_start(w_raw[0], w_rows[:, :, 0:P])
         for t in range(PACK):
             nc.sync.dma_start(x_plane[t][:], x_rows[:, t, :])
         nc.sync.dma_start(slot_sb[:], slot)
-        for b in range(2):
-            nc.sync.dma_start(w_raw[b], w_rows[:, :, b * P : (b + 1) * P])
-            nc.sync.dma_start(store[b][:], mem[b * P : (b + 1) * P, :])
-
-        warm = keep.tile([P, 2], F32, name="warm")
-        nc.gpsimd.memset(warm[:, 0:1], 0.0)
-        nc.scalar.activation(warm[:, 1:2], warm[:, 0:1], COPY)
+        nc.sync.dma_start(store[0][:], mem[0:P, :])
+        nc.sync.dma_start(w_raw[1], w_rows[:, :, P : 2 * P])
+        nc.sync.dma_start(store[1][:], mem[P : 2 * P, :])
 
         def entries(list_sb, first, last):
             return list_sb[:, first // 16 : last // 16]
 
-        x_grouped = [
-            keep.tile([P, HALF, PACK], BF16, name=f"x_grouped{h}", tag=f"x_grouped{h}", align_bytes=64) for h in range(2)
-        ]
-        picked_early = keep.tile([P, 2 * HALF], BF16, name="picked_early")
-        picked = [picked_early[:], work[:, 192:448].bitcast(BF16)]
-        for t in range(PACK):
-            pair, plane = divmod(t, 2)
-            parts = ((0, PIECE), (PIECE, HALF)) if t == PACK - 1 else ((0, HALF),)
-            for first, last in parts:
-                nc.vector.tensor_copy(x_grouped[0][:, first:last, t], x_plane[t][:].indirect(entries(offs_sb, first, last)))
-            for first, last in parts:
-                nc.scalar.activation(
-                    picked[pair][:, plane * HALF + first : plane * HALF + last],
-                    x_plane[t][:].indirect(entries(offs_sb, HALF + first, HALF + last)),
-                    COPY,
-                )
-            if t == 1:
-                nc.gpsimd.tensor_scalar(
-                    x_grouped[1][:, :, 0:2],
-                    picked[0].rearrange("p (t j) -> p j t", t=2),
-                    1.0,
-                    0.0,
-                    op0=mybir.AluOpType.mult,
-                    op1=mybir.AluOpType.add,
-                )
-        late = picked[1].rearrange("p (t j) -> p j t", t=2)
-        nc.gpsimd.tensor_scalar(
-            x_grouped[1][:, 0:PIECE, 2:4], late[:, 0:PIECE, :], 1.0, 0.0, op0=mybir.AluOpType.mult, op1=mybir.AluOpType.add
-        )
-        nc.scalar.copy(x_grouped[1][:, PIECE:HALF, 2:4], late[:, PIECE:HALF, :])
-
-        w_grouped = [
-            keep.tile([P, P, PACK], BF16, name=f"w_grouped{b}", tag=tag, align_bytes=64)
-            for b, tag in enumerate(("x_plane3", "x_grouped1"))
-        ]
+        w_grouped = [keep.tile([P, P, PACK], BF16, name=f"w_grouped{b}", align_bytes=64)[:] for b in range(2)]
         w_codes = [keep.tile([P, P], U32, name=f"w_codes{b}", align_bytes=64) for b in range(2)]
         w_scales = [keep.tile([P, P], U8, name=f"w_scales{b}", align_bytes=64) for b in range(2)]
-        x_codes = [keep.tile([P, HALF], U32, name=f"x_codes{h}", align_bytes=64) for h in range(2)]
-        x_scales = [keep.tile([P, HALF], U8, name=f"x_scales{h}", align_bytes=64) for h in range(2)]
+        x_codes = keep.tile([P, S], U32, name="x_codes", align_bytes=64)
+        x_scales = keep.tile([P, S], U8, name="x_scales", align_bytes=64)
 
-        def quantize(codes, scales, grouped):
-            nc.vector.quantize_mx(out=codes.bitcast(FP8X4), scales=scales, in_=grouped.rearrange("p j t -> p (j t)"))
+        def quantize_x(first, last):
+            nc.vector.quantize_mx(
+                out=x_codes[:, first:last].bitcast(FP8X4),
+                scales=x_scales[:, first:last],
+                in_=x_row[:, first * PACK : last * PACK],
+            )
+
+        def w_views(b):
+            return w_grouped[b].rearrange("p (c i) t -> p c t i", i=4), w_raw[b].rearrange("p t (c i) -> p c t i", i=4)
+
+        def quantize_w(b):
+            nc.vector.quantize_mx(
+                out=w_codes[b][:].bitcast(FP8X4), scales=w_scales[b][:], in_=w_grouped[b].rearrange("p n t -> p (n t)")
+            )
 
         def product(bank, column, b, first, last):
-            h, start = divmod(first, HALF)
-            cols = slice(start, start + last - first)
             nc.tensor.matmul_mx(
                 out=bank[:, column : column + last - first],
                 lhsT=w_codes[b][:].bitcast(FP8X4),
                 lhsT_scale=w_scales[b][:],
-                rhs=x_codes[h][:, cols].bitcast(FP8X4),
-                rhs_scale=x_scales[h][:, cols],
+                rhs=x_codes[:, first:last].bitcast(FP8X4),
+                rhs_scale=x_scales[:, first:last],
                 start=True,
                 stop=True,
             )
 
-        def larger(bank, first, old):
-            nc.vector.tensor_tensor(new[:, first : first + old.shape[1]], bank, old, MAX)
+        def larger(bank, first, last):
+            nc.vector.tensor_tensor(new[:, first:last], bank[:], old[:, first:last], MAX)
+
+        def look_up(engine, b, first, last):
+            target = old[:, b * S + first : b * S + last]
+            window = store[b][:].indirect(entries(slot_sb, first, last))
+            if engine is nc.scalar:
+                nc.scalar.activation(target, window, COPY)
+            else:
+                nc.vector.tensor_copy(target, window)
+
+        x_row = keep.tile([P, S * PACK], BF16, name="x_row", align_bytes=64)
+        x_grouped = x_row[:].rearrange("p (j t) -> p j t", t=PACK)
+        early = keep.tile([P, 2, STAGED], BF16, name="early")
+        parts = ((DIRECT, DIRECT + PIECE), (DIRECT + PIECE, S))
+        late = [keep.tile([P, 2, last - first], BF16, name=f"late{first}") for first, last in parts]
+
+        def gpsimd_copy(target, source):
+            nc.gpsimd.tensor_scalar(target, source, 1.0, 0.0, op0=mybir.AluOpType.mult, op1=mybir.AluOpType.add)
+
+        nc.scalar.copy(*w_views(0))
+        quantize_w(0)
+        for t in range(PACK):
+            for first, last in ((0, PIECE), (PIECE, DIRECT)) if t == PACK - 1 else ((0, DIRECT),):
+                nc.vector.tensor_copy(x_grouped[:, first:last, t], x_plane[t][:].indirect(entries(offs_sb, first, last)))
+            if t < 2:
+                nc.scalar.activation(early[:, t, :], x_plane[t][:].indirect(entries(offs_sb, DIRECT, S)), COPY)
+            else:
+                for i, (first, last) in enumerate(parts):
+                    nc.scalar.activation(late[i][:, t - 2, :], x_plane[t][:].indirect(entries(offs_sb, first, last)), COPY)
+            if t == 1:
+                gpsimd_copy(x_grouped[:, DIRECT:S, 0:2], early[:].rearrange("p t j -> p j t"))
+        gpsimd_copy(x_grouped[:, parts[0][0] : parts[0][1], 2:4], late[0][:].rearrange("p t j -> p j t"))
+        nc.scalar.copy(x_grouped[:, parts[1][0] : parts[1][1], 2:4], late[1][:].rearrange("p t j -> p j t"))
 
         banks = [psum.tile([P, width], F32, name=f"y{i}") for i, width in enumerate((128, 256, 256, 384))]
 
-        nc.vector.tensor_copy(
-            w_grouped[0][:].rearrange("p (c i) t -> p c t i", i=4), w_raw[0].rearrange("p t (c i) -> p c t i", i=4)
-        )
-        quantize(x_codes[0][:], x_scales[0][:], x_grouped[0][:])
-        quantize(w_codes[0][:], w_scales[0][:], w_grouped[0][:])
-        quantize(x_codes[1][:], x_scales[1][:], x_grouped[1][:])
+        quantize_x(0, PIECE)
+        quantize_x(PIECE, S)
         product(banks[0], 0, 0, 0, 128)
-        product(banks[1], 0, 0, 128, 256)
-        product(banks[1], 128, 0, 256, 384)
+        product(banks[1], 0, 0, 128, 384)
         product(banks[2], 0, 0, 384, 512)
 
-        nc.vector.tensor_copy(old_first[:, 0:128], store[0][:].indirect(entries(slot_sb, 0, 128)))
-        nc.vector.tensor_copy(old_first[:, 128:256], store[0][:].indirect(entries(slot_sb, 128, 256)))
-        nc.scalar.activation(old_first[:, 256:S], store[0][:].indirect(entries(slot_sb, 256, S)), COPY)
-        larger(banks[0][:], 0, old_first[:, 0:128])
+        look_up(nc.scalar, 0, 0, PIECE)
+        look_up(nc.scalar, 0, PIECE, 384)
+        look_up(nc.scalar, 0, 384, S)
+        larger(banks[0], 0, 128)
+        nc.vector.tensor_copy(*w_views(1))
         nc.scalar.activation(store[0][:].indirect(entries(slot_sb, 0, 128)), new[:, 0:128], COPY)
-        larger(banks[1][:], 128, old_first[:, 128:384])
-
-        nc.gpsimd.tensor_scalar(
-            w_grouped[1][:],
-            w_raw[1].rearrange("p t n -> p n t"),
-            1.0,
-            0.0,
-            op0=mybir.AluOpType.mult,
-            op1=mybir.AluOpType.add,
-        )
-        quantize(w_codes[1][:], w_scales[1][:], w_grouped[1][:])
+        quantize_w(1)
         product(banks[2], 128, 1, 0, 128)
-        product(banks[3], 0, 1, 128, 256)
-        product(banks[3], 128, 1, 256, 512)
+        product(banks[3], 0, 1, 128, 384)
+        product(banks[3], 256, 1, 384, 512)
 
-        nc.vector.tensor_copy(old_vector[:, 0:128], store[1][:].indirect(entries(slot_sb, 0, 128)))
-        nc.vector.tensor_copy(old_vector[:, 128:256], store[1][:].indirect(entries(slot_sb, 128, 256)))
-        nc.scalar.activation(old_scalar, store[1][:].indirect(entries(slot_sb, 256, S)), COPY)
-        larger(banks[2][:], 384, work[:, 512:768])
+        larger(banks[1], 128, 384)
+        look_up(nc.vector, 1, 0, PIECE)
+        look_up(nc.vector, 1, PIECE, VECTOR_SECOND)
+        look_up(nc.scalar, 1, VECTOR_SECOND, S)
+        larger(banks[2], 384, S + 128)
         nc.scalar.activation(store[0][:].indirect(entries(slot_sb, 128, S)), new[:, 128:S], COPY)
         nc.sync.dma_start(out[0:P, :], store[0][:])
-        larger(banks[3][:, 0:128], S + 128, old_vector[:, 128:256])
-        larger(banks[3][:, 128:384], S + 256, old_scalar)
-        nc.vector.tensor_copy(store[1][:].indirect(entries(slot_sb, 0, 128)), new[:, S : S + 128])
-        nc.vector.tensor_copy(store[1][:].indirect(entries(slot_sb, 128, S)), new[:, S + 128 : 2 * S])
+        larger(banks[3], S + 128, 2 * S)
+        nc.vector.tensor_copy(store[1][:].indirect(slot_sb[:]), new[:, S : 2 * S])
         nc.sync.dma_start(out[P : 2 * P, :], store[1][:])

@@ -16,10 +16,7 @@ MAX = mybir.AluOpType.max
 
 P = 128
 PACK = 4
-PIECE = 128
-DIRECT = 288
-STAGED = S - DIRECT
-VECTOR_SECOND = 256
+X_VECTOR = 256
 
 
 def tile_picked_idxput_max_e_kernel(tc, xT, mem, w1, offs, slot, out):
@@ -31,32 +28,31 @@ def tile_picked_idxput_max_e_kernel(tc, xT, mem, w1, offs, slot, out):
 
         offs_sb = lists.tile([P, S // 16], U16, name="offs_sb")
         slot_sb = lists.tile([P, S // 16], U16, name="slot_sb")
-        x_plane = [keep.tile([P, T], F32, name=f"x_plane{t}") for t in range(PACK)]
-        store = [keep.tile([P, U], F32, name=f"store{b}") for b in range(2)]
+        x_plane = [keep.tile([P, T], F32, name=f"x_plane{t}", align_bytes=256) for t in range(PACK)]
+        store = [keep.tile([P, U], F32, name=f"store{b}", align_bytes=256) for b in range(2)]
         old = keep.tile([P, 2 * S], F32, name="old")
         new = keep.tile([P, 2 * S], F32, name="new")
-        w_raw_first = keep.tile([P, PACK, P], F32, name="w_raw_first")
-        w_raw = [w_raw_first[:], new[:, PIECE : PIECE + S].rearrange("p (t n) -> p t n", t=PACK)]
-
-        x_rows = xT.rearrange("(p t) c -> p t c", t=PACK)
-        w_rows = w1.rearrange("(p t) n -> p t n", t=PACK)
-        nc.sync.dma_start(offs_sb[:], offs)
-        nc.sync.dma_start(w_raw[0], w_rows[:, :, 0:P])
-        for t in range(PACK):
-            nc.sync.dma_start(x_plane[t][:], x_rows[:, t, :])
-        nc.sync.dma_start(slot_sb[:], slot)
-        nc.sync.dma_start(store[0][:], mem[0:P, :])
-        nc.sync.dma_start(w_raw[1], w_rows[:, :, P : 2 * P])
-        nc.sync.dma_start(store[1][:], mem[P : 2 * P, :])
-
-        def entries(list_sb, first, last):
-            return list_sb[:, first // 16 : last // 16]
-
+        x_row = keep.tile([P, S * PACK], BF16, name="x_row", align_bytes=64)
+        x_grouped = x_row[:].rearrange("p (j t) -> p j t", t=PACK)
         w_grouped = [keep.tile([P, P, PACK], BF16, name=f"w_grouped{b}", align_bytes=64)[:] for b in range(2)]
         w_codes = [keep.tile([P, P], U32, name=f"w_codes{b}", align_bytes=64) for b in range(2)]
         w_scales = [keep.tile([P, P], U8, name=f"w_scales{b}", align_bytes=64) for b in range(2)]
         x_codes = keep.tile([P, S], U32, name="x_codes", align_bytes=64)
         x_scales = keep.tile([P, S], U8, name="x_scales", align_bytes=64)
+        x_rows = xT.rearrange("(p t) c -> p t c", t=PACK)
+        w_rows = w1.rearrange("(p t) n -> p t n", t=PACK)
+
+        def entries(list_sb, first, last):
+            return list_sb[:, first // 16 : last // 16]
+
+        def move(engine, target, source):
+            if engine is nc.scalar:
+                nc.scalar.activation(target, source, COPY)
+            else:
+                nc.vector.tensor_copy(target, source)
+
+        def pick(engine, t, first, last):
+            move(engine, x_grouped[:, first:last, t], x_plane[t][:].indirect(entries(offs_sb, first, last)))
 
         def quantize_x(first, last):
             nc.vector.quantize_mx(
@@ -65,8 +61,19 @@ def tile_picked_idxput_max_e_kernel(tc, xT, mem, w1, offs, slot, out):
                 in_=x_row[:, first * PACK : last * PACK],
             )
 
-        def w_views(b):
-            return w_grouped[b].rearrange("p (c i) t -> p c t i", i=4), w_raw[b].rearrange("p t (c i) -> p c t i", i=4)
+        def round_w(engine, b, first, last):
+            target = w_grouped[b][:, first:last, :]
+            source = w_raw[b][:, :, first:last]
+            if engine is nc.gpsimd:
+                nc.gpsimd.tensor_scalar(
+                    target, source.rearrange("p t n -> p n t"), 1.0, 0.0, op0=mybir.AluOpType.mult, op1=mybir.AluOpType.add
+                )
+            else:
+                views = target.rearrange("p (c i) t -> p c t i", i=4), source.rearrange("p t (c i) -> p c t i", i=4)
+                if engine is nc.scalar:
+                    nc.scalar.copy(*views)
+                else:
+                    nc.vector.tensor_copy(*views)
 
         def quantize_w(b):
             nc.vector.quantize_mx(
@@ -88,63 +95,57 @@ def tile_picked_idxput_max_e_kernel(tc, xT, mem, w1, offs, slot, out):
             nc.vector.tensor_tensor(new[:, first:last], bank[:], old[:, first:last], MAX)
 
         def look_up(engine, b, first, last):
-            target = old[:, b * S + first : b * S + last]
-            window = store[b][:].indirect(entries(slot_sb, first, last))
-            if engine is nc.scalar:
-                nc.scalar.activation(target, window, COPY)
-            else:
-                nc.vector.tensor_copy(target, window)
+            move(engine, old[:, b * S + first : b * S + last], store[b][:].indirect(entries(slot_sb, first, last)))
 
-        x_row = keep.tile([P, S * PACK], BF16, name="x_row", align_bytes=64)
-        x_grouped = x_row[:].rearrange("p (j t) -> p j t", t=PACK)
-        early = keep.tile([P, 2, STAGED], BF16, name="early")
-        parts = ((DIRECT, DIRECT + PIECE), (DIRECT + PIECE, S))
-        late = [keep.tile([P, 2, last - first], BF16, name=f"late{first}") for first, last in parts]
+        def put(engine, b, first, last):
+            move(engine, store[b][:].indirect(entries(slot_sb, first, last)), new[:, b * S + first : b * S + last])
 
-        def gpsimd_copy(target, source):
-            nc.gpsimd.tensor_scalar(target, source, 1.0, 0.0, op0=mybir.AluOpType.mult, op1=mybir.AluOpType.add)
+        w_raw = [keep.tile([P, PACK, P], F32, name=f"w_raw{b}", align_bytes=256)[:] for b in range(2)]
 
-        nc.scalar.copy(*w_views(0))
+        nc.sync.dma_start(offs_sb[:], offs)
+        nc.sync.dma_start(w_raw[0], w_rows[:, :, 0:P])
+        for t in range(PACK):
+            nc.sync.dma_start(x_plane[t][:], x_rows[:, t, :])
+        nc.sync.dma_start(slot_sb[:], slot)
+        nc.sync.dma_start(store[0][:], mem[0:P, :])
+        nc.sync.dma_start(w_raw[1], w_rows[:, :, P : 2 * P])
+        nc.sync.dma_start(store[1][:], mem[P : 2 * P, :])
+
+        round_w(nc.scalar, 0, 0, P)
         quantize_w(0)
         for t in range(PACK):
-            for first, last in ((0, PIECE), (PIECE, DIRECT)) if t == PACK - 1 else ((0, DIRECT),):
-                nc.vector.tensor_copy(x_grouped[:, first:last, t], x_plane[t][:].indirect(entries(offs_sb, first, last)))
-            if t < 2:
-                nc.scalar.activation(early[:, t, :], x_plane[t][:].indirect(entries(offs_sb, DIRECT, S)), COPY)
-            else:
-                for i, (first, last) in enumerate(parts):
-                    nc.scalar.activation(late[i][:, t - 2, :], x_plane[t][:].indirect(entries(offs_sb, first, last)), COPY)
-            if t == 1:
-                gpsimd_copy(x_grouped[:, DIRECT:S, 0:2], early[:].rearrange("p t j -> p j t"))
-        gpsimd_copy(x_grouped[:, parts[0][0] : parts[0][1], 2:4], late[0][:].rearrange("p t j -> p j t"))
-        nc.scalar.copy(x_grouped[:, parts[1][0] : parts[1][1], 2:4], late[1][:].rearrange("p t j -> p j t"))
+            for first, last in ((0, 128), (128, X_VECTOR)) if t == PACK - 1 else ((0, X_VECTOR),):
+                pick(nc.vector, t, first, last)
+            pick(nc.scalar, t, X_VECTOR, S)
+        quantize_x(0, 128)
+        quantize_x(128, 512)
 
-        banks = [psum.tile([P, width], F32, name=f"y{i}") for i, width in enumerate((128, 256, 256, 384))]
-
-        quantize_x(0, PIECE)
-        quantize_x(PIECE, S)
+        banks = [psum.tile([P, width], F32, name=f"y{i}") for i, width in enumerate((128, 320, 192, 128, 256))]
         product(banks[0], 0, 0, 0, 128)
         product(banks[1], 0, 0, 128, 384)
-        product(banks[2], 0, 0, 384, 512)
+        product(banks[1], 256, 0, 384, 448)
+        product(banks[2], 0, 0, 448, 512)
 
-        look_up(nc.scalar, 0, 0, PIECE)
-        look_up(nc.scalar, 0, PIECE, 384)
-        look_up(nc.scalar, 0, 384, S)
+        look_up(nc.scalar, 0, 0, 128)
+        look_up(nc.scalar, 0, 256, 512)
         larger(banks[0], 0, 128)
-        nc.vector.tensor_copy(*w_views(1))
-        nc.scalar.activation(store[0][:].indirect(entries(slot_sb, 0, 128)), new[:, 0:128], COPY)
+        look_up(nc.vector, 0, 128, 256)
+        put(nc.scalar, 0, 0, 128)
+        larger(banks[1], 128, 448)
+        round_w(nc.gpsimd, 1, 0, P)
         quantize_w(1)
-        product(banks[2], 128, 1, 0, 128)
-        product(banks[3], 0, 1, 128, 384)
-        product(banks[3], 256, 1, 384, 512)
-
-        larger(banks[1], 128, 384)
-        look_up(nc.vector, 1, 0, PIECE)
-        look_up(nc.vector, 1, PIECE, VECTOR_SECOND)
-        look_up(nc.scalar, 1, VECTOR_SECOND, S)
-        larger(banks[2], 384, S + 128)
-        nc.scalar.activation(store[0][:].indirect(entries(slot_sb, 128, S)), new[:, 128:S], COPY)
+        product(banks[3], 0, 1, 384, 512)
+        product(banks[2], 64, 1, 0, 128)
+        product(banks[4], 0, 1, 128, 384)
+        look_up(nc.vector, 1, 384, 512)
+        look_up(nc.vector, 1, 256, 384)
+        look_up(nc.scalar, 1, 0, 128)
+        look_up(nc.scalar, 1, 128, 256)
+        larger(banks[3], S + 384, 2 * S)
+        larger(banks[2], 448, S + 128)
+        larger(banks[4], S + 128, S + 384)
+        put(nc.scalar, 1, 384, 512)
+        put(nc.vector, 0, 128, S)
         nc.sync.dma_start(out[0:P, :], store[0][:])
-        larger(banks[3], S + 128, 2 * S)
-        nc.vector.tensor_copy(store[1][:].indirect(slot_sb[:]), new[:, S : 2 * S])
+        put(nc.scalar, 1, 0, 384)
         nc.sync.dma_start(out[P : 2 * P, :], store[1][:])

@@ -102,8 +102,8 @@ def tile_picked_idxput_max_e_kernel(tc, xT, mem, w1, offs, slot, out):
 
         w_raw = [keep.tile([P, PACK, P], F32, name=f"w_raw{b}", align_bytes=256)[:] for b in range(2)]
 
-        nc.sync.dma_start(offs_sb[:], offs)
         nc.sync.dma_start(w_raw[0], w_rows[:, :, 0:P])
+        nc.sync.dma_start(offs_sb[:], offs)
         for t in range(PACK):
             nc.sync.dma_start(x_plane[t][:], x_rows[:, t, :])
         nc.sync.dma_start(slot_sb[:], slot)
@@ -120,32 +120,28 @@ def tile_picked_idxput_max_e_kernel(tc, xT, mem, w1, offs, slot, out):
         quantize_x(0, 128)
         quantize_x(128, 512)
 
-        banks = [psum.tile([P, width], F32, name=f"y{i}") for i, width in enumerate((128, 320, 192, 128, 256))]
+        banks = [psum.tile([P, width], F32, name=f"y{i}") for i, width in enumerate((128, 256, 256, 384))]
         product(banks[0], 0, 0, 0, 128)
         product(banks[1], 0, 0, 128, 384)
-        product(banks[1], 256, 0, 384, 448)
-        product(banks[2], 0, 0, 448, 512)
+        product(banks[2], 0, 0, 384, 512)
 
         look_up(nc.scalar, 0, 0, 128)
         look_up(nc.scalar, 0, 256, 512)
         larger(banks[0], 0, 128)
         look_up(nc.vector, 0, 128, 256)
         put(nc.scalar, 0, 0, 128)
-        larger(banks[1], 128, 448)
+        larger(banks[1], 128, 384)
         round_w(nc.gpsimd, 1, 0, P)
         quantize_w(1)
-        product(banks[3], 0, 1, 384, 512)
-        product(banks[2], 64, 1, 0, 128)
-        product(banks[4], 0, 1, 128, 384)
-        look_up(nc.vector, 1, 384, 512)
-        look_up(nc.vector, 1, 256, 384)
-        look_up(nc.scalar, 1, 0, 128)
-        look_up(nc.scalar, 1, 128, 256)
-        larger(banks[3], S + 384, 2 * S)
-        larger(banks[2], 448, S + 128)
-        larger(banks[4], S + 128, S + 384)
-        put(nc.scalar, 1, 384, 512)
-        put(nc.vector, 0, 128, S)
+        product(banks[2], 128, 1, 0, 128)
+        product(banks[3], 0, 1, 128, 384)
+        product(banks[3], 256, 1, 384, 512)
+        look_up(nc.vector, 1, 0, 128)
+        look_up(nc.vector, 1, 128, 256)
+        look_up(nc.scalar, 1, 256, 512)
+        larger(banks[2], 384, S + 128)
+        put(nc.scalar, 0, 128, S)
         nc.sync.dma_start(out[0:P, :], store[0][:])
-        put(nc.scalar, 1, 0, 384)
+        larger(banks[3], S + 128, 2 * S)
+        put(nc.vector, 1, 0, S)
         nc.sync.dma_start(out[P : 2 * P, :], store[1][:])

@@ -16,7 +16,7 @@ MAX = mybir.AluOpType.max
 
 P = 128
 PACK = 4
-X_VECTOR = 256
+X_VECTOR = (384, 384, 256, 256)
 
 
 def tile_picked_idxput_max_e_kernel(tc, xT, mem, w1, offs, slot, out):
@@ -30,7 +30,7 @@ def tile_picked_idxput_max_e_kernel(tc, xT, mem, w1, offs, slot, out):
         slot_sb = lists.tile([P, S // 16], U16, name="slot_sb")
         x_plane = [keep.tile([P, T], F32, name=f"x_plane{t}", align_bytes=256) for t in range(PACK)]
         store = [keep.tile([P, U], F32, name=f"store{b}", align_bytes=256) for b in range(2)]
-        old = keep.tile([P, 2 * S], F32, name="old")
+        old = keep.tile([P, 2 * S], F32, name="old", align_bytes=256)
         new = keep.tile([P, 2 * S], F32, name="new")
         x_row = keep.tile([P, S * PACK], BF16, name="x_row", align_bytes=64)
         x_grouped = x_row[:].rearrange("p (j t) -> p j t", t=PACK)
@@ -91,57 +91,61 @@ def tile_picked_idxput_max_e_kernel(tc, xT, mem, w1, offs, slot, out):
                 stop=True,
             )
 
-        def larger(bank, first, last):
-            nc.vector.tensor_tensor(new[:, first:last], bank[:], old[:, first:last], MAX)
+        def larger(bank, first, last, place):
+            nc.vector.tensor_tensor(new[:, first:last], bank[:], old[:, place : place + last - first], MAX)
 
-        def look_up(engine, b, first, last):
-            move(engine, old[:, b * S + first : b * S + last], store[b][:].indirect(entries(slot_sb, first, last)))
+        def look_up(engine, b, first, last, place):
+            move(engine, old[:, place : place + last - first], store[b][:].indirect(entries(slot_sb, first, last)))
 
         def put(engine, b, first, last):
             move(engine, store[b][:].indirect(entries(slot_sb, first, last)), new[:, b * S + first : b * S + last])
 
-        w_raw = [keep.tile([P, PACK, P], F32, name=f"w_raw{b}", align_bytes=256)[:] for b in range(2)]
+        w_all = old[:].rearrange("p (t n) -> p t n", t=PACK)
+        w_raw = [w_all[:, :, b * P : (b + 1) * P] for b in range(2)]
 
-        nc.sync.dma_start(w_raw[0], w_rows[:, :, 0:P])
+        nc.sync.dma_start(x_plane[0][:], x_rows[:, 0, :])
         nc.sync.dma_start(offs_sb[:], offs)
-        for t in range(PACK):
+        for t in range(1, PACK):
             nc.sync.dma_start(x_plane[t][:], x_rows[:, t, :])
+        nc.sync.dma_start(w_all, w_rows)
         nc.sync.dma_start(slot_sb[:], slot)
         nc.sync.dma_start(store[0][:], mem[0:P, :])
-        nc.sync.dma_start(w_raw[1], w_rows[:, :, P : 2 * P])
         nc.sync.dma_start(store[1][:], mem[P : 2 * P, :])
 
-        round_w(nc.scalar, 0, 0, P)
-        quantize_w(0)
         for t in range(PACK):
-            for first, last in ((0, 128), (128, X_VECTOR)) if t == PACK - 1 else ((0, X_VECTOR),):
+            for first, last in ((0, 128), (128, X_VECTOR[t])) if t == PACK - 1 else ((0, X_VECTOR[t]),):
                 pick(nc.vector, t, first, last)
-            pick(nc.scalar, t, X_VECTOR, S)
+            pick(nc.scalar, t, X_VECTOR[t], S)
         quantize_x(0, 128)
         quantize_x(128, 512)
+        round_w(nc.scalar, 0, 0, P)
+        round_w(nc.vector, 1, 0, 64)
+        round_w(nc.scalar, 1, 64, P)
+        quantize_w(0)
+        quantize_w(1)
 
-        banks = [psum.tile([P, width], F32, name=f"y{i}") for i, width in enumerate((128, 256, 256, 384))]
+        banks = [psum.tile([P, width], F32, name=f"y{i}") for i, width in enumerate((128, 320, 192, 384))]
         product(banks[0], 0, 0, 0, 128)
         product(banks[1], 0, 0, 128, 384)
-        product(banks[2], 0, 0, 384, 512)
-
-        look_up(nc.scalar, 0, 0, 128)
-        look_up(nc.scalar, 0, 256, 512)
-        larger(banks[0], 0, 128)
-        look_up(nc.vector, 0, 128, 256)
-        put(nc.scalar, 0, 0, 128)
-        larger(banks[1], 128, 384)
-        round_w(nc.gpsimd, 1, 0, P)
-        quantize_w(1)
-        product(banks[2], 128, 1, 0, 128)
+        product(banks[1], 256, 0, 384, 448)
+        product(banks[2], 0, 0, 448, 512)
+        product(banks[2], 64, 1, 0, 128)
         product(banks[3], 0, 1, 128, 384)
         product(banks[3], 256, 1, 384, 512)
-        look_up(nc.vector, 1, 0, 128)
-        look_up(nc.vector, 1, 128, 256)
-        look_up(nc.scalar, 1, 256, 512)
-        larger(banks[2], 384, S + 128)
+
+        look_up(nc.scalar, 0, 0, 128, 512)
+        look_up(nc.vector, 0, 128, 384, 64)
+        look_up(nc.scalar, 0, 384, 512, 320)
+        larger(banks[0], 0, 128, 512)
+        put(nc.scalar, 0, 0, 128)
+        larger(banks[1], 128, 448, 64)
+        look_up(nc.vector, 1, 0, 128, 448)
+        look_up(nc.vector, 1, 128, 288, 576)
+        look_up(nc.scalar, 1, 288, 512, 64)
+        larger(banks[2], 448, S + 128, 384)
         put(nc.scalar, 0, 128, S)
         nc.sync.dma_start(out[0:P, :], store[0][:])
-        larger(banks[3], S + 128, 2 * S)
+        larger(banks[3][:, 0:160], S + 128, S + 288, 576)
+        larger(banks[3][:, 160:384], S + 288, 2 * S, 64)
         put(nc.vector, 1, 0, S)
         nc.sync.dma_start(out[P : 2 * P, :], store[1][:])

@@ -16,7 +16,7 @@ MAX = mybir.AluOpType.max
 
 P = 128
 PACK = 4
-X_VECTOR = (384, 384, 256, 256)
+X_VECTOR = (256, 256, 256, 256)
 
 
 def tile_picked_idxput_max_e_kernel(tc, xT, mem, w1, offs, slot, out):
@@ -111,6 +111,10 @@ def tile_picked_idxput_max_e_kernel(tc, xT, mem, w1, offs, slot, out):
         nc.sync.dma_start(slot_sb[:], slot)
         nc.sync.dma_start(store[0][:], mem[0:P, :])
         nc.sync.dma_start(store[1][:], mem[P : 2 * P, :])
+
+        warm = keep.tile([P, 2], F32, name="warm")
+        nc.gpsimd.memset(warm[:, 0:1], 0.0)
+        nc.scalar.activation(warm[:, 1:2], warm[:, 0:1], COPY)
 
         for t in range(PACK):
             for first, last in ((0, 128), (128, X_VECTOR[t])) if t == PACK - 1 else ((0, X_VECTOR[t]),):

@@ -28,8 +28,8 @@ def tile_picked_idxput_max_e_kernel(tc, xT, mem, w1, offs, slot, out):
 
         offs_sb = lists.tile([P, S // 16], U16, name="offs_sb")
         slot_sb = lists.tile([P, S // 16], U16, name="slot_sb")
-        x_plane = [keep.tile([P, T], F32, name=f"x_plane{t}", align_bytes=256) for t in range(PACK)]
-        store = [keep.tile([P, U], F32, name=f"store{b}", align_bytes=256) for b in range(2)]
+        x_plane = [keep.tile([P, T], F32, name=f"x_plane{t}", tag=f"rows{t}", align_bytes=256) for t in range(PACK)]
+        store = [keep.tile([P, U], F32, name="store0", align_bytes=256)]
         old = keep.tile([P, 2 * S], F32, name="old", align_bytes=256)
         new = keep.tile([P, 2 * S], F32, name="new")
         x_row = keep.tile([P, S * PACK], BF16, name="x_row", align_bytes=64)
@@ -103,14 +103,12 @@ def tile_picked_idxput_max_e_kernel(tc, xT, mem, w1, offs, slot, out):
         w_all = old[:].rearrange("p (t n) -> p t n", t=PACK)
         w_raw = [w_all[:, :, b * P : (b + 1) * P] for b in range(2)]
 
-        nc.sync.dma_start(x_plane[0][:], x_rows[:, 0, :])
         nc.sync.dma_start(offs_sb[:], offs)
-        for t in range(1, PACK):
-            nc.sync.dma_start(x_plane[t][:], x_rows[:, t, :])
-        nc.sync.dma_start(w_all, w_rows)
         nc.sync.dma_start(slot_sb[:], slot)
-        nc.sync.dma_start(store[0][:], mem[0:P, :])
-        nc.sync.dma_start(store[1][:], mem[P : 2 * P, :])
+        for t in range(PACK):
+            nc.scalar.dma_start(x_plane[t][:], x_rows[:, t, :])
+        nc.scalar.dma_start(w_all, w_rows)
+        nc.scalar.dma_start(store[0][:], mem[0:P, :])
 
         warm = keep.tile([P, 2], F32, name="warm")
         nc.gpsimd.memset(warm[:, 0:1], 0.0)
@@ -120,6 +118,9 @@ def tile_picked_idxput_max_e_kernel(tc, xT, mem, w1, offs, slot, out):
             for first, last in ((0, 128), (128, X_VECTOR[t])) if t == PACK - 1 else ((0, X_VECTOR[t]),):
                 pick(nc.vector, t, first, last)
             pick(nc.scalar, t, X_VECTOR[t], S)
+            if t == 0:
+                store.append(keep.tile([P, U], F32, name="store1", tag="rows0", align_bytes=256))
+                nc.scalar.dma_start(store[1][:], mem[P : 2 * P, :])
         quantize_x(0, 128)
         quantize_x(128, 512)
         round_w(nc.scalar, 0, 0, P)

@@ -138,19 +138,20 @@ def tile_picked_idxput_max_e_kernel(tc, xT, mem, w1, offs, slot, out):
         product(banks[3], 0, 1, 128, 384)
         product(banks[3], 256, 1, 384, 512)
 
-        look_up(nc.scalar, 0, 0, 128, 512)
-        look_up(nc.vector, 0, 128, 384, 64)
-        look_up(nc.scalar, 0, 384, 512, 320)
-        larger(banks[0], 0, 128, 512)
+        look_up(nc.scalar, 0, 0, 128, 0)
+        look_up(nc.vector, 0, 288, 512, 288)
+        look_up(nc.scalar, 0, 128, 288, 128)
+        larger(banks[0], 0, 128, 0)
         put(nc.scalar, 0, 0, 128)
-        larger(banks[1], 128, 448, 64)
-        look_up(nc.vector, 1, 0, 128, 448)
-        look_up(nc.vector, 1, 128, 288, 576)
-        look_up(nc.scalar, 1, 288, 512, 64)
-        larger(banks[2], 448, S + 128, 384)
+        larger(banks[1][:, 0:160], 128, 288, 128)
+        larger(banks[1][:, 160:320], 288, 448, 288)
+        look_up(nc.vector, 1, 0, 128, S)
+        look_up(nc.vector, 1, 128, 288, S + 128)
+        look_up(nc.scalar, 1, 288, 512, S + 288)
+        larger(banks[2], 448, S + 128, 448)
         put(nc.scalar, 0, 128, S)
         nc.sync.dma_start(out[0:P, :], store[0][:])
-        larger(banks[3][:, 0:160], S + 128, S + 288, 576)
-        larger(banks[3][:, 160:384], S + 288, 2 * S, 64)
+        larger(banks[3][:, 0:160], S + 128, S + 288, S + 128)
+        larger(banks[3][:, 160:384], S + 288, 2 * S, S + 288)
         put(nc.vector, 1, 0, S)
         nc.sync.dma_start(out[P : 2 * P, :], store[1][:])

@@ -139,19 +139,21 @@ def tile_picked_idxput_max_e_kernel(tc, xT, mem, w1, offs, slot, out):
         product(banks[3], 256, 1, 384, 512)
 
         look_up(nc.scalar, 0, 0, 128, 0)
-        look_up(nc.vector, 0, 288, 512, 288)
-        look_up(nc.scalar, 0, 128, 288, 128)
+        look_up(nc.vector, 0, 256, 512, 256)
+        look_up(nc.scalar, 0, 128, 256, 128)
         larger(banks[0], 0, 128, 0)
         put(nc.scalar, 0, 0, 128)
-        larger(banks[1][:, 0:160], 128, 288, 128)
-        larger(banks[1][:, 160:320], 288, 448, 288)
+        larger(banks[1][:, 0:128], 128, 256, 128)
+        larger(banks[1][:, 128:320], 256, 448, 256)
         look_up(nc.vector, 1, 0, 128, S)
         look_up(nc.vector, 1, 128, 288, S + 128)
-        look_up(nc.scalar, 1, 288, 512, S + 288)
+        look_up(nc.scalar, 1, 288, 416, S + 288)
+        look_up(nc.scalar, 1, 416, 512, S + 416)
         larger(banks[2], 448, S + 128, 448)
         put(nc.scalar, 0, 128, S)
         nc.sync.dma_start(out[0:P, :], store[0][:])
         larger(banks[3][:, 0:160], S + 128, S + 288, S + 128)
-        larger(banks[3][:, 160:384], S + 288, 2 * S, S + 288)
+        larger(banks[3][:, 160:288], S + 288, S + 416, S + 288)
+        larger(banks[3][:, 288:384], S + 416, 2 * S, S + 416)
         put(nc.vector, 1, 0, S)
         nc.sync.dma_start(out[P : 2 * P, :], store[1][:])

@@ -139,21 +139,21 @@ def tile_picked_idxput_max_e_kernel(tc, xT, mem, w1, offs, slot, out):
         product(banks[3], 256, 1, 384, 512)
 
         look_up(nc.scalar, 0, 0, 128, 0)
-        look_up(nc.vector, 0, 256, 512, 256)
-        look_up(nc.scalar, 0, 128, 256, 128)
+        look_up(nc.vector, 0, 288, 512, 288)
+        look_up(nc.scalar, 0, 128, 288, 128)
         larger(banks[0], 0, 128, 0)
         put(nc.scalar, 0, 0, 128)
-        larger(banks[1][:, 0:128], 128, 256, 128)
-        larger(banks[1][:, 128:320], 256, 448, 256)
+        larger(banks[1][:, 0:160], 128, 288, 128)
+        larger(banks[1][:, 160:320], 288, 448, 288)
         look_up(nc.vector, 1, 0, 128, S)
-        look_up(nc.vector, 1, 128, 288, S + 128)
-        look_up(nc.scalar, 1, 288, 416, S + 288)
-        look_up(nc.scalar, 1, 416, 512, S + 416)
+        look_up(nc.vector, 1, 128, 256, S + 128)
+        look_up(nc.scalar, 1, 256, 384, S + 256)
+        look_up(nc.scalar, 1, 384, 512, S + 384)
         larger(banks[2], 448, S + 128, 448)
         put(nc.scalar, 0, 128, S)
         nc.sync.dma_start(out[0:P, :], store[0][:])
-        larger(banks[3][:, 0:160], S + 128, S + 288, S + 128)
-        larger(banks[3][:, 160:288], S + 288, S + 416, S + 288)
-        larger(banks[3][:, 288:384], S + 416, 2 * S, S + 416)
+        larger(banks[3][:, 0:128], S + 128, S + 256, S + 128)
+        larger(banks[3][:, 128:256], S + 256, S + 384, S + 256)
+        larger(banks[3][:, 256:384], S + 384, 2 * S, S + 384)
         put(nc.vector, 1, 0, S)
         nc.sync.dma_start(out[P : 2 * P, :], store[1][:])

from contextlib import ExitStack

import concourse.mybir as mybir

K, T, S, N, U = 512, 1024, 512, 256, 1024
FLOPS = 2 * K * S * N

F32 = mybir.dt.float32
BF16 = mybir.dt.bfloat16
U32 = mybir.dt.uint32
U16 = mybir.dt.uint16
U8 = mybir.dt.uint8
FP8X4 = mybir.dt.float8_e4m3fn_x4
COPY = mybir.ActivationFunctionType.Copy
MAX = mybir.AluOpType.max

P = 128
PACK = 4
X_VECTOR = (256, 256, 256, 256)


def tile_picked_idxput_max_e_kernel(tc, xT, mem, w1, offs, slot, out):
    nc = tc.nc
    with ExitStack() as ctx:
        lists = ctx.enter_context(tc.tile_pool(name="lists", bufs=1))
        keep = ctx.enter_context(tc.tile_pool(name="keep", bufs=1))
        psum = ctx.enter_context(tc.psum_pool(name="psum", bufs=1))

        offs_sb = lists.tile([P, S // 16], U16, name="offs_sb")
        slot_sb = lists.tile([P, S // 16], U16, name="slot_sb")
        x_plane = [keep.tile([P, T], F32, name=f"x_plane{t}", tag=f"rows{t}", align_bytes=256) for t in range(PACK)]
        store = [keep.tile([P, U], F32, name="store0", align_bytes=256)]
        old = keep.tile([P, 2 * S], F32, name="old", align_bytes=256)
        new = keep.tile([P, 2 * S], F32, name="new")
        x_row = keep.tile([P, S * PACK], BF16, name="x_row", align_bytes=64)
        x_grouped = x_row[:].rearrange("p (j t) -> p j t", t=PACK)
        w_grouped = [keep.tile([P, P, PACK], BF16, name=f"w_grouped{b}", align_bytes=64)[:] for b in range(2)]
        w_codes = [keep.tile([P, P], U32, name=f"w_codes{b}", align_bytes=64) for b in range(2)]
        w_scales = [keep.tile([P, P], U8, name=f"w_scales{b}", align_bytes=64) for b in range(2)]
        x_codes = keep.tile([P, S], U32, name="x_codes", align_bytes=64)
        x_scales = keep.tile([P, S], U8, name="x_scales", align_bytes=64)
        x_rows = xT.rearrange("(p t) c -> p t c", t=PACK)
        w_rows = w1.rearrange("(p t) n -> p t n", t=PACK)

        def entries(list_sb, first, last):
            return list_sb[:, first // 16 : last // 16]

        def move(engine, target, source):
            if engine is nc.scalar:
                nc.scalar.activation(target, source, COPY)
            else:
                nc.vector.tensor_copy(target, source)

        def pick(engine, t, first, last):
            move(engine, x_grouped[:, first:last, t], x_plane[t][:].indirect(entries(offs_sb, first, last)))

        def quantize_x(first, last):
            nc.vector.quantize_mx(
                out=x_codes[:, first:last].bitcast(FP8X4),
                scales=x_scales[:, first:last],
                in_=x_row[:, first * PACK : last * PACK],
            )

        def round_w(engine, b, first, last):
            target = w_grouped[b][:, first:last, :]
            source = w_raw[b][:, :, first:last]
            if engine is nc.gpsimd:
                nc.gpsimd.tensor_scalar(
                    target, source.rearrange("p t n -> p n t"), 1.0, 0.0, op0=mybir.AluOpType.mult, op1=mybir.AluOpType.add
                )
            else:
                views = target.rearrange("p (c i) t -> p c t i", i=4), source.rearrange("p t (c i) -> p c t i", i=4)
                if engine is nc.scalar:
                    nc.scalar.copy(*views)
                else:
                    nc.vector.tensor_copy(*views)

        def quantize_w(b):
            nc.vector.quantize_mx(
                out=w_codes[b][:].bitcast(FP8X4), scales=w_scales[b][:], in_=w_grouped[b].rearrange("p n t -> p (n t)")
            )

        def product(bank, column, b, first, last):
            nc.tensor.matmul_mx(
                out=bank[:, column : column + last - first],
                lhsT=w_codes[b][:].bitcast(FP8X4),
                lhsT_scale=w_scales[b][:],
                rhs=x_codes[:, first:last].bitcast(FP8X4),
                rhs_scale=x_scales[:, first:last],
                start=True,
                stop=True,
            )

        def larger(bank, first, last, place):
            nc.vector.tensor_tensor(new[:, first:last], bank[:], old[:, place : place + last - first], MAX)

        def look_up(engine, b, first, last, place):
            move(engine, old[:, place : place + last - first], store[b][:].indirect(entries(slot_sb, first, last)))

        def put(engine, b, first, last):
            move(engine, store[b][:].indirect(entries(slot_sb, first, last)), new[:, b * S + first : b * S + last])

        w_all = old[:].rearrange("p (t n) -> p t n", t=PACK)
        w_raw = [w_all[:, :, b * P : (b + 1) * P] for b in range(2)]

        nc.sync.dma_start(offs_sb[:], offs)
        nc.sync.dma_start(slot_sb[:], slot)
        for t in range(PACK):
            nc.scalar.dma_start(x_plane[t][:], x_rows[:, t, :])
        nc.scalar.dma_start(w_all, w_rows)
        nc.scalar.dma_start(store[0][:], mem[0:P, :])

        warm = keep.tile([P, 2], F32, name="warm")
        nc.gpsimd.memset(warm[:, 0:1], 0.0)
        nc.scalar.activation(warm[:, 1:2], warm[:, 0:1], COPY)

        for t in range(PACK):
            for first, last in ((0, 128), (128, X_VECTOR[t])) if t == PACK - 1 else ((0, X_VECTOR[t]),):
                pick(nc.vector, t, first, last)
            pick(nc.scalar, t, X_VECTOR[t], S)
            if t == 0:
                store.append(keep.tile([P, U], F32, name="store1", tag="rows0", align_bytes=256))
                nc.scalar.dma_start(store[1][:], mem[P : 2 * P, :])
        quantize_x(0, 128)
        quantize_x(128, 512)
        round_w(nc.scalar, 0, 0, P)
        round_w(nc.vector, 1, 0, 64)
        round_w(nc.scalar, 1, 64, P)
        quantize_w(0)
        quantize_w(1)

        banks = [psum.tile([P, width], F32, name=f"y{i}") for i, width in enumerate((128, 320, 192, 384))]
        product(banks[0], 0, 0, 0, 128)
        product(banks[1], 0, 0, 128, 384)
        product(banks[1], 256, 0, 384, 448)
        product(banks[2], 0, 0, 448, 512)
        product(banks[2], 64, 1, 0, 128)
        product(banks[3], 0, 1, 128, 384)
        product(banks[3], 256, 1, 384, 512)

        look_up(nc.scalar, 0, 0, 128, 0)
        look_up(nc.vector, 0, 288, 512, 288)
        look_up(nc.scalar, 0, 128, 288, 128)
        larger(banks[0], 0, 128, 0)
        put(nc.scalar, 0, 0, 128)
        larger(banks[1][:, 0:160], 128, 288, 128)
        larger(banks[1][:, 160:320], 288, 448, 288)
        look_up(nc.vector, 1, 0, 128, S)
        look_up(nc.vector, 1, 128, 256, S + 128)
        look_up(nc.scalar, 1, 256, 384, S + 256)
        look_up(nc.scalar, 1, 384, 512, S + 384)
        larger(banks[2], 448, S + 128, 448)
        put(nc.scalar, 0, 128, S)
        nc.sync.dma_start(out[0:P, :], store[0][:])
        larger(banks[3][:, 0:128], S + 128, S + 256, S + 128)
        larger(banks[3][:, 128:256], S + 256, S + 384, S + 256)
        larger(banks[3][:, 256:384], S + 384, 2 * S, S + 384)
        put(nc.vector, 1, 0, S)
        nc.sync.dma_start(out[P : 2 * P, :], store[1][:])
